import numpy as np
import ml_dtypes


def mxq(x, axis, fmt="e4m3"):
    dtype, down = {"e4m3": (ml_dtypes.float8_e4m3fn, 7), "e5m2": (ml_dtypes.float8_e5m2, 14)}[fmt]
    v = np.moveaxis(np.asarray(x, np.float32).astype(ml_dtypes.bfloat16).astype(np.float64), axis, -1)
    blocks = v.reshape(v.shape[:-1] + (-1, 32))
    amax = np.abs(blocks).max(-1, keepdims=True)
    byte = np.maximum(np.where(amax > 0, np.frexp(amax)[1] - 1 + 127, 0) - down, 1)
    scale = np.exp2(byte - 127.0)
    codes = (blocks / scale).astype(np.float32).astype(dtype).astype(np.float64)
    return np.moveaxis((codes * scale).reshape(v.shape), -1, axis)


WIDE = False


def mx_kscale(k):
    if not WIDE:
        return np.ones(k)
    levels = np.array([10, -10, 5, -5, 0])
    if k % 512:
        return np.exp2(np.random.permutation(np.resize(levels, k // 32))).repeat(32)
    a = np.empty((k // 512, 16))
    for p in range(k // 512):
        a[p, :8] = np.random.permutation(np.resize(levels, 8))
        for g in range(8):
            far = levels[np.abs(levels - a[p, g]) >= 10]
            a[p, g + 8] = far[np.random.randint(len(far))]
    return np.exp2(a.ravel()).repeat(32)


def f64(x):
    return np.asarray(x).astype(np.float64)


def striped(idx):
    return np.tile(np.asarray(idx).reshape(-1, 16).T, (8, 1)).astype(np.uint16)


def unstriped(offs):
    return offs[:16].T.reshape(-1).astype(np.int64)


E2M1 = np.array([0.0, 0.5, 1.0, 1.5, 2.0, 3.0, 4.0, 6.0, -0.0, -0.5, -1.0, -1.5, -2.0, -3.0, -4.0, -6.0])


def pack_weight(w, fmt):
    k, n = w.shape
    w = f64(np.asarray(w, np.float32).astype(ml_dtypes.bfloat16)).reshape(k // 32, 32, n)
    amax = np.abs(w).max(1)
    if fmt == "e4m3":
        byte = np.frexp(amax)[1] - 1 + 127 - 7
    else:
        mant, ex = np.frexp(amax / 6.0)
        byte = np.where(mant > 0.5, ex, ex - 1) + 127
    byte = np.clip(np.where(amax > 0, byte, 1), 1, 254)
    scaled = (w * np.exp2(127.0 - byte)[:, None, :]).reshape(k, n).astype(np.float32)
    by_word = np.ascontiguousarray(scaled.reshape(k // 512, 128, 4, n).transpose(0, 1, 3, 2))
    if fmt == "e4m3":
        words = by_word.astype(ml_dtypes.float8_e4m3fn).view(np.uint8)
    else:
        c = by_word.astype(ml_dtypes.float4_e2m1fn).view(np.uint8) & 0xF
        words = (c[..., 0::2] | (c[..., 1::2] << 4)).reshape(k // 512, 128, 2 * n)
    return np.ascontiguousarray(words), np.ascontiguousarray(byte.astype(np.uint8).reshape(k // 512, 16, n))


def unpack_weight(words, scales, fmt):
    g, _, n = scales.shape
    words = np.ascontiguousarray(words).reshape(g, 128, n, -1)
    if fmt == "e4m3":
        vals = words.view(ml_dtypes.float8_e4m3fn).astype(np.float64)
    else:
        nib = np.empty((g, 128, n, 4), np.uint8)
        nib[..., 0::2] = words & 0xF
        nib[..., 1::2] = words >> 4
        vals = E2M1[nib]
    vals = vals * np.repeat(np.exp2(scales.astype(np.float64) - 127.0), 8, axis=1)[..., None]
    return vals.transpose(0, 1, 3, 2).reshape(g * 512, n)


def silu(v):
    return v / (1.0 + np.exp(-v))


def bf(x):
    return np.asarray(x, np.float32).astype(ml_dtypes.bfloat16)


def planes(Y):
    r, m = Y.shape
    b = f64(bf(Y)).reshape(r // 32, 32, m)
    amax = np.abs(b).max(1)
    byte = np.clip(np.where(amax > 0, np.frexp(amax)[1] - 1 + 127 - 7, 1), 1, 254)
    codes = (b * np.exp2(127.0 - byte)[:, None, :]).reshape(r, m).astype(np.float32).astype(ml_dtypes.float8_e4m3fn).view(np.uint8)
    words = codes.reshape(r // 512, 128, 4, m).transpose(0, 1, 3, 2)
    return np.ascontiguousarray(words), np.ascontiguousarray(byte.astype(np.uint8).reshape(r // 512, 16, m))


B, N, T, D, NQ = 1, 512, 2048, 1024, 512


def setup_inputs():
    n = np.random.standard_normal
    idx = np.random.permutation(T)[:B * N]
    s = mx_kscale(D)[:, None]
    kp = pack_weight(n((D, T)) / s, "e2m1")
    cp = pack_weight(n((D, T)) / s, "e2m1")
    return {
        "qT": (n((B, D, NQ)) * s * (1.00 / np.sqrt(D))).astype(np.float32),
        "k_words": np.ascontiguousarray(kp[0].reshape(1, 2, 128, T, 2).transpose(0, 2, 3, 1, 4)).reshape(1, 128, T, 4),
        "k_scales": kp[1],
        "c_words": np.ascontiguousarray(cp[0].reshape(1, 2, 128, T, 2).transpose(0, 2, 3, 1, 4)).reshape(1, 128, T, 4),
        "c_scales": cp[1],
        "offs": striped(idx),
    }


def reference(qT, k_words, k_scales, c_words, c_scales, offs):
    idx = unstriped(offs)
    pick = lambda x, which: x[:, which].reshape(x.shape[0], B, -1).transpose(1, 0, 2)
    k = unpack_weight(k_words.reshape(1, 128, T, 2, 2).transpose(0, 3, 1, 2, 4).reshape(2, 128, 2 * T), k_scales, "e2m1")
    kg = pick(k, idx)
    c = unpack_weight(c_words.reshape(1, 128, T, 2, 2).transpose(0, 3, 1, 2, 4).reshape(2, 128, 2 * T), c_scales, "e2m1")
    cg = pick(c, idx)
    qq = mxq(f64(qT), 1, "e4m3")
    a = kg.transpose(0, 2, 1) @ qq
    z = cg.transpose(0, 2, 1) @ qq
    y = silu(a) * z
    Y = y[0]
    words, scales = planes(Y)
    return Y, words, scales

@@ -1,0 +1,202 @@
+from contextlib import ExitStack
+
+import concourse.mybir as mybir
+
+T, D, NQ, SLOTS = 2048, 1024, 512, 512
+FLOPS = 2 * 2 * SLOTS * D * NQ
+
+F32 = mybir.dt.float32
+BF16 = mybir.dt.bfloat16
+I32 = mybir.dt.int32
+U32 = mybir.dt.uint32
+U16 = mybir.dt.uint16
+U8 = mybir.dt.uint8
+FP8X4 = mybir.dt.float8_e4m3fn_x4
+FP4X4 = mybir.dt.float4_e2m1fn_x4
+SILU = mybir.ActivationFunctionType.Silu
+MULT = mybir.AluOpType.mult
+
+P = 128
+PACK = 4
+PASSES = 2
+CH = 128
+CHUNKS = NQ // CH
+ROW0 = 96
+
+
+def interleave(copy, dst, src):
+    copy(
+        dst.rearrange("p (c i) t -> p c t i", i=4),
+        src.rearrange("p t (c i) -> p c t i", i=4),
+    )
+
+
+def tile_attend_plh_swiglu4_topk_kernel(tc, qT, k_words, k_scales, c_words, c_scales, offs, out_0, out_1, out_2):
+    nc = tc.nc
+    with ExitStack() as ctx:
+        lists = ctx.enter_context(tc.tile_pool(name="lists", bufs=1))
+        keep = ctx.enter_context(tc.tile_pool(name="keep", bufs=1))
+        psum = ctx.enter_context(tc.psum_pool(name="psum", bufs=1))
+
+        offsets = lists.tile([P, SLOTS // 16], U16, name="offsets")
+        nc.sync.dma_start(offsets[:], offs)
+
+        warm = keep.tile([P, 8], F32, name="warm")
+        warm_out = keep.tile([P, 8], F32, name="warm_out")
+        nc.vector.memset(warm[:], 0.0)
+        nc.scalar.activation(warm_out[:], warm[:], SILU)
+
+        swin = []
+        for name, scales in (("ks", k_scales), ("cs", c_scales)):
+            w = keep.tile([P, T], U8, name=name, align_bytes=64)
+            nc.sync.dma_start(w[ROW0:P, :].bitcast(I32), scales.rearrange("o f t -> f o t").bitcast(I32))
+            nc.vector.memset(w[0:ROW0, :].bitcast(I32), 0)
+            swin.append(w)
+        planes = keep.tile([P, PASSES, 2, SLOTS], U8, name="planes", align_bytes=64)
+        nc.vector.memset(planes[:].rearrange("p o w s -> p (o w s)").bitcast(I32), 0)
+
+        def load_words(name, words):
+            w = keep.tile([P, T], U32, name=name, tag=name, align_bytes=64)
+            nc.sync.dma_start(w[:].bitcast(I32), words[0].rearrange("p t b -> p (t b)").bitcast(I32))
+            return w
+
+        def load_q(dst, c, o):
+            rows = qT[0, 512 * o : 512 * (o + 1), c * CH : (c + 1) * CH]
+            nc.sync.dma_start(dst, rows.rearrange("(p j) n -> p j n", j=PACK))
+
+        qraw = {}
+        kw = load_words("kw", k_words)
+        for o in range(PASSES):
+            t = keep.tile([P, PACK, CH], F32, name="q0_%d" % o)
+            load_q(t[:], 0, o)
+            qraw[0, o] = t[:]
+        cw = load_words("cw", c_words)
+        for o in range(PASSES):
+            t = keep.tile([P, PACK, CH], F32, name="q1_%d" % o)
+            load_q(t[:], 1, o)
+            qraw[1, o] = t[:]
+
+        dealt = keep.tile([P, 2, SLOTS], U8, name="dealt", align_bytes=64)
+        gs = []
+        for w in range(2):
+            g = keep.tile([P, SLOTS], U8, name="gs%d" % w, align_bytes=64)
+            nc.vector.tensor_copy(g[:], swin[w][:].indirect(offsets[:]))
+            gs.append(g)
+        for w in range(2):
+            nc.vector.tensor_copy(
+                dealt[:, w, :].rearrange("p (r c i) -> p c r i", r=PACK, i=16),
+                gs[w][:].rearrange("p (c i r) -> p c r i", r=PACK, i=16),
+            )
+        for Q in range(4):
+            nc.scalar.dma_start(
+                planes[32 * Q : 32 * Q + 4].rearrange("p o w s -> p o (w s)").bitcast(I32),
+                dealt[ROW0 + 8 * Q : ROW0 + 8 * Q + 8].rearrange("p w s -> p (w s)").bitcast(I32),
+            )
+
+        def gather_words(name, win):
+            g = keep.tile([P, SLOTS], U32, name=name + "_g", align_bytes=64)
+            nc.vector.tensor_copy(g[:], win[:].indirect(offsets[:]))
+            return g
+
+        def split_words(name, g):
+            w = keep.tile([P, PASSES * SLOTS * 2], U8, name=name + "_w", align_bytes=64)
+            nc.vector.tensor_copy(
+                w[:].bitcast(U16).rearrange("p (h r c i) -> p h c r i", h=PASSES, r=PACK, i=4),
+                g[:].bitcast(U16).rearrange("p (c i r h) -> p h c r i", h=PASSES, r=PACK, i=4),
+            )
+            return w
+
+        kg = gather_words("k", kw)
+        qtail = keep.tile([P, 4, PACK * CH], F32, name="qtail", tag="kw", align_bytes=64)
+        for c in (2, 3):
+            for o in range(PASSES):
+                dst = qtail[:, 2 * (c - 2) + o, :].rearrange("p (j n) -> p j n", j=PACK)
+                load_q(dst, c, o)
+                qraw[c, o] = dst
+        weights = [split_words("k", kg)]
+
+        qcodes = keep.tile([P, CHUNKS, PASSES, CH], U32, name="qcodes", align_bytes=64)
+        qscales = keep.tile([P, CHUNKS, PASSES, CH], U8, name="qscales", align_bytes=64)
+        ycodes = keep.tile([P, NQ], U32, name="ycodes", align_bytes=64)
+        yscales = keep.tile([P, NQ], U8, name="yscales", align_bytes=64)
+
+        def cast_q(c, engines):
+            qb = keep.tile([P, PASSES, CH, PACK], BF16, name="qb%d" % c, align_bytes=64)
+            for o in range(PASSES):
+                interleave(engines[o], qb[:, o], qraw[c, o])
+            return qb
+
+        def quant_q(c, qb, split):
+            if split:
+                for o in range(PASSES):
+                    nc.vector.quantize_mx(
+                        out=qcodes[:, c, o, :].bitcast(FP8X4),
+                        scales=qscales[:, c, o, :],
+                        in_=qb[:, o].rearrange("p n t -> p (n t)"),
+                    )
+            else:
+                nc.vector.quantize_mx(
+                    out=qcodes[:, c].rearrange("p o n -> p (o n)").bitcast(FP8X4),
+                    scales=qscales[:, c].rearrange("p o n -> p (o n)"),
+                    in_=qb[:].rearrange("p o n t -> p (o n t)"),
+                )
+
+        def products(c, w):
+            acc = psum.tile([P, PACK, CH], F32, name="acc%d_%d" % (w, c))
+            for r in range(PACK):
+                for o in range(PASSES):
+                    col = o * SLOTS + r * P
+                    nc.tensor.matmul_mx(
+                        out=acc[:, r, :],
+                        lhsT=weights[w][:, 2 * col : 2 * (col + P)].bitcast(FP4X4),
+                        lhsT_scale=planes[:, o, w, r * P : (r + 1) * P],
+                        rhs=qcodes[:, c, o, :].bitcast(FP8X4),
+                        rhs_scale=qscales[:, c, o, :],
+                        start=(o == 0),
+                        stop=(o == PASSES - 1),
+                    )
+            return acc
+
+        def gate(c):
+            a = products(c, 0)
+            s = keep.tile([P, PACK, CH], F32, name="s%d" % c)
+            nc.scalar.activation(s[:], a[:], SILU)
+            return s
+
+        def finish(c, s, ycopy):
+            z = products(c, 1)
+            cols = slice(c * CH, (c + 1) * CH)
+            y = keep.tile([P, PACK, CH], F32, name="y%d" % c)
+            nc.vector.tensor_tensor(y[:], z[:], s[:], MULT)
+            nc.sync.dma_start(out_0[:, cols].rearrange("(p r) n -> p r n", r=PACK), y[:])
+            yb = keep.tile([P, CH, PACK], BF16, name="yb%d" % c, align_bytes=64)
+            interleave(ycopy, yb[:], y[:])
+            nc.vector.quantize_mx(
+                out=ycodes[:, cols].bitcast(FP8X4), scales=yscales[:, cols], in_=yb[:].rearrange("p n t -> p (n t)")
+            )
+            nc.sync.dma_start(
+                out_1[0, :, cols, :].rearrange("p n b -> p (n b)").bitcast(I32), ycodes[:, cols].bitcast(I32)
+            )
+
+        S, V = nc.scalar.copy, nc.vector.tensor_copy
+        qb0 = cast_q(0, (S, S))
+        quant_q(0, qb0, False)
+        s0 = gate(0)
+        cg = gather_words("c", cw)
+        weights.append(split_words("c", cg))
+        qb1 = cast_q(1, (S, S))
+        quant_q(1, qb1, False)
+        finish(0, s0, V)
+        s1 = gate(1)
+        qb2 = cast_q(2, (S, S))
+        quant_q(2, qb2, False)
+        finish(1, s1, V)
+        s2 = gate(2)
+        qb3 = cast_q(3, (S, S))
+        quant_q(3, qb3, True)
+        finish(2, s2, V)
+        s3 = gate(3)
+        finish(3, s3, V)
+        for Q in range(4):
+            eng = nc.scalar if Q % 2 else nc.sync
+            eng.dma_start(out_2[0, 4 * Q : 4 * Q + 4, :].bitcast(I32), yscales[32 * Q : 32 * Q + 4, :].bitcast(I32))

@@ -41,45 +41,38 @@ def tile_attend_plh_swiglu4_topk_kernel(tc, qT, k_words, k_scales, c_words, c_sc
         offsets = lists.tile([P, SLOTS // 16], U16, name="offsets")
         nc.sync.dma_start(offsets[:], offs)
 
-        warm = keep.tile([P, 8], F32, name="warm")
-        warm_out = keep.tile([P, 8], F32, name="warm_out")
-        nc.vector.memset(warm[:], 0.0)
-        nc.scalar.activation(warm_out[:], warm[:], SILU)
-
         swin = []
         for name, scales in (("ks", k_scales), ("cs", c_scales)):
             w = keep.tile([P, T], U8, name=name, align_bytes=64)
-            nc.sync.dma_start(w[ROW0:P, :].bitcast(I32), scales.rearrange("o f t -> f o t").bitcast(I32))
+            nc.scalar.dma_start(w[ROW0:P, :].bitcast(I32), scales.rearrange("o f t -> f o t").bitcast(I32))
             nc.vector.memset(w[0:ROW0, :].bitcast(I32), 0)
             swin.append(w)
         planes = keep.tile([P, PASSES, 2, SLOTS], U8, name="planes", align_bytes=64)
         nc.vector.memset(planes[:].rearrange("p o w s -> p (o w s)").bitcast(I32), 0)
 
-        def load_words(name, words):
-            w = keep.tile([P, T], U32, name=name, tag=name, align_bytes=64)
+        warm = keep.tile([P, 8], F32, name="warm")
+        warm_out = keep.tile([P, 8], F32, name="warm_out")
+        nc.gpsimd.memset(warm[:], 0.0)
+        nc.scalar.activation(warm_out[:], warm[:], SILU)
+
+        def load_words(name, words, tag):
+            w = keep.tile([P, T], U32, name=name, tag=tag, align_bytes=64)
             nc.sync.dma_start(w[:].bitcast(I32), words[0].rearrange("p t b -> p (t b)").bitcast(I32))
             return w
 
-        def load_q(dst, c, o):
-            rows = qT[0, 512 * o : 512 * (o + 1), c * CH : (c + 1) * CH]
-            nc.sync.dma_start(dst, rows.rearrange("(p j) n -> p j n", j=PACK))
+        def load_q(o):
+            t = keep.tile([P, PACK, NQ], F32, name="qraw%d" % o)
+            nc.sync.dma_start(t[:], qT[0, 512 * o : 512 * (o + 1), :].rearrange("(p j) n -> p j n", j=PACK))
+            return t
 
-        qraw = {}
-        kw = load_words("kw", k_words)
-        for o in range(PASSES):
-            t = keep.tile([P, PACK, CH], F32, name="q0_%d" % o)
-            load_q(t[:], 0, o)
-            qraw[0, o] = t[:]
-        cw = load_words("cw", c_words)
-        for o in range(PASSES):
-            t = keep.tile([P, PACK, CH], F32, name="q1_%d" % o)
-            load_q(t[:], 1, o)
-            qraw[1, o] = t[:]
+        qraw0 = load_q(0)
+        kw = load_words("kw", k_words, "kw")
+        qraw1 = load_q(1)
 
         dealt = keep.tile([P, 2, SLOTS], U8, name="dealt", align_bytes=64)
         gs = []
         for w in range(2):
-            g = keep.tile([P, SLOTS], U8, name="gs%d" % w, align_bytes=64)
+            g = keep.tile([P, SLOTS], U8, name="gs%d" % w, tag="gs%d" % w, align_bytes=64)
             nc.vector.tensor_copy(g[:], swin[w][:].indirect(offsets[:]))
             gs.append(g)
         for w in range(2):
@@ -88,115 +81,101 @@ def tile_attend_plh_swiglu4_topk_kernel(tc, qT, k_words, k_scales, c_words, c_sc
                 gs[w][:].rearrange("p (c i r) -> p c r i", r=PACK, i=16),
             )
         for Q in range(4):
-            nc.scalar.dma_start(
+            nc.sync.dma_start(
                 planes[32 * Q : 32 * Q + 4].rearrange("p o w s -> p o (w s)").bitcast(I32),
                 dealt[ROW0 + 8 * Q : ROW0 + 8 * Q + 8].rearrange("p w s -> p (w s)").bitcast(I32),
             )
+        cw = load_words("cw", c_words, "gs1")
 
         def gather_words(name, win):
             g = keep.tile([P, SLOTS], U32, name=name + "_g", align_bytes=64)
             nc.vector.tensor_copy(g[:], win[:].indirect(offsets[:]))
-            return g
+            src = g[:].bitcast(U16).rearrange("p (c i r h) -> p h c r i", h=PASSES, r=PACK, i=4)
+            pairs = []
+            for u in range(2):
+                w = keep.tile([P, PASSES * 2 * P * 2], U8, name="%s_w%d" % (name, u), align_bytes=64)
+                nc.vector.tensor_copy(
+                    w[:].bitcast(U16).rearrange("p (h r c i) -> p h c r i", h=PASSES, r=2, i=4),
+                    src[:, :, :, 2 * u : 2 * u + 2, :],
+                )
+                pairs.append(w)
+            return pairs
 
-        def split_words(name, g):
-            w = keep.tile([P, PASSES * SLOTS * 2], U8, name=name + "_w", align_bytes=64)
-            nc.vector.tensor_copy(
-                w[:].bitcast(U16).rearrange("p (h r c i) -> p h c r i", h=PASSES, r=PACK, i=4),
-                g[:].bitcast(U16).rearrange("p (c i r h) -> p h c r i", h=PASSES, r=PACK, i=4),
-            )
-            return w
-
-        kg = gather_words("k", kw)
-        qtail = keep.tile([P, 4, PACK * CH], F32, name="qtail", tag="kw", align_bytes=64)
-        for c in (2, 3):
-            for o in range(PASSES):
-                dst = qtail[:, 2 * (c - 2) + o, :].rearrange("p (j n) -> p j n", j=PACK)
-                load_q(dst, c, o)
-                qraw[c, o] = dst
-        weights = [split_words("k", kg)]
-
-        qcodes = keep.tile([P, CHUNKS, PASSES, CH], U32, name="qcodes", align_bytes=64)
-        qscales = keep.tile([P, CHUNKS, PASSES, CH], U8, name="qscales", align_bytes=64)
+        qcodes = keep.tile([P, PASSES, NQ], U32, name="qcodes", align_bytes=64)
+        qscales = keep.tile([P, PASSES, NQ], U8, name="qscales", align_bytes=64)
         ycodes = keep.tile([P, NQ], U32, name="ycodes", align_bytes=64)
         yscales = keep.tile([P, NQ], U8, name="yscales", align_bytes=64)
+        S, V = nc.scalar.copy, nc.vector.tensor_copy
 
-        def cast_q(c, engines):
-            qb = keep.tile([P, PASSES, CH, PACK], BF16, name="qb%d" % c, align_bytes=64)
-            for o in range(PASSES):
-                interleave(engines[o], qb[:, o], qraw[c, o])
-            return qb
-
-        def quant_q(c, qb, split):
-            if split:
-                for o in range(PASSES):
-                    nc.vector.quantize_mx(
-                        out=qcodes[:, c, o, :].bitcast(FP8X4),
-                        scales=qscales[:, c, o, :],
-                        in_=qb[:, o].rearrange("p n t -> p (n t)"),
-                    )
-            else:
+        def quantise_q(o, raw):
+            qb = keep.tile([P, NQ, PACK], BF16, name="qb%d" % o, align_bytes=64)
+            halves = (slice(0, NQ // 2), slice(NQ // 2, NQ))
+            interleave(S, qb[:, halves[1], :], raw[:, :, halves[1]])
+            interleave(V, qb[:, halves[0], :], raw[:, :, halves[0]])
+            for cols in halves:
                 nc.vector.quantize_mx(
-                    out=qcodes[:, c].rearrange("p o n -> p (o n)").bitcast(FP8X4),
-                    scales=qscales[:, c].rearrange("p o n -> p (o n)"),
-                    in_=qb[:].rearrange("p o n t -> p (o n t)"),
+                    out=qcodes[:, o, cols].bitcast(FP8X4),
+                    scales=qscales[:, o, cols],
+                    in_=qb[:, cols, :].rearrange("p n t -> p (n t)"),
                 )
 
-        def products(c, w):
-            acc = psum.tile([P, PACK, CH], F32, name="acc%d_%d" % (w, c))
-            for r in range(PACK):
-                for o in range(PASSES):
-                    col = o * SLOTS + r * P
-                    nc.tensor.matmul_mx(
-                        out=acc[:, r, :],
-                        lhsT=weights[w][:, 2 * col : 2 * (col + P)].bitcast(FP4X4),
-                        lhsT_scale=planes[:, o, w, r * P : (r + 1) * P],
-                        rhs=qcodes[:, c, o, :].bitcast(FP8X4),
-                        rhs_scale=qscales[:, c, o, :],
-                        start=(o == 0),
-                        stop=(o == PASSES - 1),
-                    )
-            return acc
-
-        def gate(c):
-            a = products(c, 0)
-            s = keep.tile([P, PACK, CH], F32, name="s%d" % c)
-            nc.scalar.activation(s[:], a[:], SILU)
-            return s
-
-        def finish(c, s, ycopy):
-            z = products(c, 1)
-            cols = slice(c * CH, (c + 1) * CH)
-            y = keep.tile([P, PACK, CH], F32, name="y%d" % c)
-            nc.vector.tensor_tensor(y[:], z[:], s[:], MULT)
-            nc.sync.dma_start(out_0[:, cols].rearrange("(p r) n -> p r n", r=PACK), y[:])
-            yb = keep.tile([P, CH, PACK], BF16, name="yb%d" % c, align_bytes=64)
-            interleave(ycopy, yb[:], y[:])
-            nc.vector.quantize_mx(
-                out=ycodes[:, cols].bitcast(FP8X4), scales=yscales[:, cols], in_=yb[:].rearrange("p n t -> p (n t)")
+        def one_pass(acc, pairs, w, r, o):
+            col = (o * 2 + r % 2) * P
+            nc.tensor.matmul_mx(
+                out=acc[:],
+                lhsT=pairs[r // 2][:, 2 * col : 2 * (col + P)].bitcast(FP4X4),
+                lhsT_scale=planes[:, o, w, r * P : (r + 1) * P],
+                rhs=qcodes[:, o, :].bitcast(FP8X4),
+                rhs_scale=qscales[:, o, :],
+                start=(o == 0),
+                stop=(o == PASSES - 1),
             )
+
+        quantise_q(0, qraw0)
+        kpairs = gather_words("k", kw)
+        a = [psum.tile([P, NQ], F32, name="a%d" % r) for r in range(PACK)]
+        for r in range(PACK):
+            one_pass(a[r], kpairs, 0, r, 0)
+        quantise_q(1, qraw1)
+        s = keep.tile([P, PACK, NQ], F32, name="s")
+        for r in range(PACK):
+            one_pass(a[r], kpairs, 0, r, 1)
+            nc.scalar.activation(s[:, r, :], a[r][:], SILU)
+
+        cpairs = gather_words("c", cw)
+        y = keep.tile([P, PACK, NQ], F32, name="y")
+        yb = keep.tile([P, NQ, PACK], BF16, name="yb", align_bytes=64)
+        out_rows = out_0.rearrange("(p r) n -> p r n", r=PACK)
+        first, second, rest = slice(0, CH), slice(CH, 2 * CH), slice(2 * CH, NQ)
+        for r in range(PACK):
+            z = psum.tile([P, NQ], F32, name="z%d" % r)
+            for o in range(PASSES):
+                one_pass(z, cpairs, 1, r, o)
+            for cols in (slice(0, NQ),) if r < PACK - 1 else (first, rest, second):
+                nc.vector.tensor_tensor(y[:, r, cols], z[:, cols], s[:, r, cols], MULT)
+            nc.sync.dma_start(out_rows[:, r, :], y[:, r, :])
+
+        def quantise_y(cols):
+            nc.vector.quantize_mx(
+                out=ycodes[:, cols].bitcast(FP8X4),
+                scales=yscales[:, cols],
+                in_=yb[:, cols, :].rearrange("p n t -> p (n t)"),
+            )
+
+        def store_codes(cols):
             nc.sync.dma_start(
                 out_1[0, :, cols, :].rearrange("p n b -> p (n b)").bitcast(I32), ycodes[:, cols].bitcast(I32)
             )
 
-        S, V = nc.scalar.copy, nc.vector.tensor_copy
-        qb0 = cast_q(0, (S, S))
-        quant_q(0, qb0, False)
-        s0 = gate(0)
-        cg = gather_words("c", cw)
-        weights.append(split_words("c", cg))
-        qb1 = cast_q(1, (S, S))
-        quant_q(1, qb1, False)
-        finish(0, s0, V)
-        s1 = gate(1)
-        qb2 = cast_q(2, (S, S))
-        quant_q(2, qb2, False)
-        finish(1, s1, V)
-        s2 = gate(2)
-        qb3 = cast_q(3, (S, S))
-        quant_q(3, qb3, True)
-        finish(2, s2, V)
-        s3 = gate(3)
-        finish(3, s3, V)
+        interleave(S, yb[:, first, :], y[:, :, first])
+        interleave(S, yb[:, second, :], y[:, :, second])
+        interleave(V, yb[:, rest, :], y[:, :, rest])
+        quantise_y(first)
+        quantise_y(rest)
+        store_codes(rest)
+        quantise_y(second)
+        store_codes(slice(0, 2 * CH))
         for Q in range(4):
-            eng = nc.scalar if Q % 2 else nc.sync
-            eng.dma_start(out_2[0, 4 * Q : 4 * Q + 4, :].bitcast(I32), yscales[32 * Q : 32 * Q + 4, :].bitcast(I32))
+            nc.scalar.dma_start(
+                out_2[0, 4 * Q : 4 * Q + 4, :].bitcast(I32), yscales[32 * Q : 32 * Q + 4, :].bitcast(I32)
+            )

@@ -43,12 +43,15 @@ def tile_attend_plh_swiglu4_topk_kernel(tc, qT, k_words, k_scales, c_words, c_sc
 
         swin = []
         for name, scales in (("ks", k_scales), ("cs", c_scales)):
-            w = keep.tile([P, T], U8, name=name, align_bytes=64)
-            nc.scalar.dma_start(w[ROW0:P, :].bitcast(I32), scales.rearrange("o f t -> f o t").bitcast(I32))
+            w = keep.tile([P, T], U8, name=name, tag=name, align_bytes=64)
+            nc.sync.dma_start(w[ROW0:P, :].bitcast(I32), scales.rearrange("o f t -> f o t").bitcast(I32))
             nc.vector.memset(w[0:ROW0, :].bitcast(I32), 0)
             swin.append(w)
-        planes = keep.tile([P, PASSES, 2, SLOTS], U8, name="planes", align_bytes=64)
-        nc.vector.memset(planes[:].rearrange("p o w s -> p (o w s)").bitcast(I32), 0)
+        planes = []
+        for w in range(2):
+            plane = keep.tile([P, PASSES, SLOTS], U8, name="planes%d" % w, align_bytes=64)
+            nc.vector.memset(plane[:].rearrange("p o s -> p (o s)").bitcast(I32), 0)
+            planes.append(plane)
 
         warm = keep.tile([P, 8], F32, name="warm")
         warm_out = keep.tile([P, 8], F32, name="warm_out")
@@ -60,32 +63,36 @@ def tile_attend_plh_swiglu4_topk_kernel(tc, qT, k_words, k_scales, c_words, c_sc
             nc.sync.dma_start(w[:].bitcast(I32), words[0].rearrange("p t b -> p (t b)").bitcast(I32))
             return w
 
-        def load_q(o):
-            t = keep.tile([P, PACK, NQ], F32, name="qraw%d" % o)
+        def load_q(o, tag):
+            t = keep.tile([P, PACK, NQ], F32, name="qraw%d" % o, tag=tag, align_bytes=64)
             nc.sync.dma_start(t[:], qT[0, 512 * o : 512 * (o + 1), :].rearrange("(p j) n -> p j n", j=PACK))
             return t
 
-        qraw0 = load_q(0)
+        qraw0 = load_q(0, "qraw0")
         kw = load_words("kw", k_words, "kw")
-        qraw1 = load_q(1)
 
-        dealt = keep.tile([P, 2, SLOTS], U8, name="dealt", align_bytes=64)
-        gs = []
-        for w in range(2):
+        def gather_scales(w):
             g = keep.tile([P, SLOTS], U8, name="gs%d" % w, tag="gs%d" % w, align_bytes=64)
             nc.vector.tensor_copy(g[:], swin[w][:].indirect(offsets[:]))
-            gs.append(g)
-        for w in range(2):
+            return g
+
+        def scale_planes(w, g, queues):
+            dealt = keep.tile([P, SLOTS], U8, name="dealt%d" % w, align_bytes=64)
             nc.vector.tensor_copy(
-                dealt[:, w, :].rearrange("p (r c i) -> p c r i", r=PACK, i=16),
-                gs[w][:].rearrange("p (c i r) -> p c r i", r=PACK, i=16),
+                dealt[:].rearrange("p (r c i) -> p c r i", r=PACK, i=16),
+                g[:].rearrange("p (c i r) -> p c r i", r=PACK, i=16),
             )
-        for Q in range(4):
-            nc.sync.dma_start(
-                planes[32 * Q : 32 * Q + 4].rearrange("p o w s -> p o (w s)").bitcast(I32),
-                dealt[ROW0 + 8 * Q : ROW0 + 8 * Q + 8].rearrange("p w s -> p (w s)").bitcast(I32),
-            )
-        cw = load_words("cw", c_words, "gs1")
+            for Q in range(4):
+                queues[Q % 2].dma_start(
+                    planes[w][32 * Q : 32 * Q + 4].bitcast(I32),
+                    dealt[ROW0 + 8 * Q : ROW0 + 8 * Q + 8, :].bitcast(I32),
+                )
+
+        scale_planes(0, gather_scales(0), (nc.sync, nc.scalar))
+        qraw1 = load_q(1, "gs0")
+        cg = gather_scales(1)
+        cw = load_words("cw", c_words, "cs")
+        scale_planes(1, cg, (nc.sync, nc.sync))
 
         def gather_words(name, win):
             g = keep.tile([P, SLOTS], U32, name=name + "_g", align_bytes=64)
@@ -124,7 +131,7 @@ def tile_attend_plh_swiglu4_topk_kernel(tc, qT, k_words, k_scales, c_words, c_sc
             nc.tensor.matmul_mx(
                 out=acc[:],
                 lhsT=pairs[r // 2][:, 2 * col : 2 * (col + P)].bitcast(FP4X4),
-                lhsT_scale=planes[:, o, w, r * P : (r + 1) * P],
+                lhsT_scale=planes[w][:, o, r * P : (r + 1) * P],
                 rhs=qcodes[:, o, :].bitcast(FP8X4),
                 rhs_scale=qscales[:, o, :],
                 start=(o == 0),

@@ -2,7 +2,7 @@ from contextlib import ExitStack
 
 import concourse.mybir as mybir
 
-T, D, NQ, SLOTS = 2048, 1024, 512, 512
+NEURONS, D, NQ, SLOTS = 2048, 1024, 512, 512
 FLOPS = 2 * 2 * SLOTS * D * NQ
 
 F32 = mybir.dt.float32
@@ -18,10 +18,11 @@ MULT = mybir.AluOpType.mult
 
 P = 128
 PACK = 4
-PASSES = 2
-CH = 128
-CHUNKS = NQ // CH
-ROW0 = 96
+K_PASS = P * PACK
+PASSES = D // K_PASS
+QUADS = 4
+SCALE_ROW0 = P - 32
+GATE, LAYER = 0, 1
 
 
 def interleave(copy, dst, src):
@@ -41,148 +42,146 @@ def tile_attend_plh_swiglu4_topk_kernel(tc, qT, k_words, k_scales, c_words, c_sc
         offsets = lists.tile([P, SLOTS // 16], U16, name="offsets")
         nc.sync.dma_start(offsets[:], offs)
 
-        swin = []
-        for name, scales in (("ks", k_scales), ("cs", c_scales)):
-            w = keep.tile([P, T], U8, name=name, tag=name, align_bytes=64)
-            nc.sync.dma_start(w[ROW0:P, :].bitcast(I32), scales.rearrange("o f t -> f o t").bitcast(I32))
-            nc.vector.memset(w[0:ROW0, :].bitcast(I32), 0)
-            swin.append(w)
+        scale_tables = []
+        for name, scales in (("k_scales", k_scales), ("c_scales", c_scales)):
+            table = keep.tile([P, NEURONS], U8, name=name, tag=name, align_bytes=64)
+            nc.sync.dma_start(table[SCALE_ROW0:P, :].bitcast(I32), scales.rearrange("o f t -> f o t").bitcast(I32))
+            nc.vector.memset(table[0:SCALE_ROW0, :].bitcast(I32), 0)
+            scale_tables.append(table)
+
         planes = []
-        for w in range(2):
+        for w in (GATE, LAYER):
             plane = keep.tile([P, PASSES, SLOTS], U8, name="planes%d" % w, align_bytes=64)
             nc.vector.memset(plane[:].rearrange("p o s -> p (o s)").bitcast(I32), 0)
             planes.append(plane)
 
-        warm = keep.tile([P, 8], F32, name="warm")
-        warm_out = keep.tile([P, 8], F32, name="warm_out")
-        nc.gpsimd.memset(warm[:], 0.0)
-        nc.scalar.activation(warm_out[:], warm[:], SILU)
-
         def load_words(name, words, tag):
-            w = keep.tile([P, T], U32, name=name, tag=tag, align_bytes=64)
-            nc.sync.dma_start(w[:].bitcast(I32), words[0].rearrange("p t b -> p (t b)").bitcast(I32))
-            return w
+            table = keep.tile([P, NEURONS], U32, name=name, tag=tag, align_bytes=64)
+            nc.sync.dma_start(table[:].bitcast(I32), words[0].rearrange("p t b -> p (t b)").bitcast(I32))
+            return table
 
         def load_q(o, tag):
-            t = keep.tile([P, PACK, NQ], F32, name="qraw%d" % o, tag=tag, align_bytes=64)
-            nc.sync.dma_start(t[:], qT[0, 512 * o : 512 * (o + 1), :].rearrange("(p j) n -> p j n", j=PACK))
-            return t
-
-        qraw0 = load_q(0, "qraw0")
-        kw = load_words("kw", k_words, "kw")
+            raw = keep.tile([P, PACK, NQ], F32, name="q_raw%d" % o, tag=tag, align_bytes=64)
+            rows = qT[0, K_PASS * o : K_PASS * (o + 1), :]
+            nc.sync.dma_start(raw[:], rows.rearrange("(p j) n -> p j n", j=PACK))
+            return raw
 
         def gather_scales(w):
-            g = keep.tile([P, SLOTS], U8, name="gs%d" % w, tag="gs%d" % w, align_bytes=64)
-            nc.vector.tensor_copy(g[:], swin[w][:].indirect(offsets[:]))
-            return g
+            name = "scales_gathered%d" % w
+            gathered = keep.tile([P, SLOTS], U8, name=name, tag=name, align_bytes=64)
+            nc.vector.tensor_copy(gathered[:], scale_tables[w][:].indirect(offsets[:]))
+            return gathered
 
-        def scale_planes(w, g, queues):
-            dealt = keep.tile([P, SLOTS], U8, name="dealt%d" % w, align_bytes=64)
+        def fill_planes(w, gathered, tag):
+            dealt = keep.tile([P, SLOTS], U8, name="scales_dealt%d" % w, tag=tag, align_bytes=64)
             nc.vector.tensor_copy(
                 dealt[:].rearrange("p (r c i) -> p c r i", r=PACK, i=16),
-                g[:].rearrange("p (c i r) -> p c r i", r=PACK, i=16),
+                gathered[:].rearrange("p (c i r) -> p c r i", r=PACK, i=16),
             )
-            for Q in range(4):
-                queues[Q % 2].dma_start(
-                    planes[w][32 * Q : 32 * Q + 4].bitcast(I32),
-                    dealt[ROW0 + 8 * Q : ROW0 + 8 * Q + 8, :].bitcast(I32),
+            for quad in range(QUADS):
+                first_row = SCALE_ROW0 + 8 * quad
+                nc.sync.dma_start(
+                    planes[w][32 * quad : 32 * quad + 4].bitcast(I32),
+                    dealt[first_row : first_row + 8, :].bitcast(I32),
                 )
 
-        scale_planes(0, gather_scales(0), (nc.sync, nc.scalar))
-        qraw1 = load_q(1, "gs0")
-        cg = gather_scales(1)
-        cw = load_words("cw", c_words, "cs")
-        scale_planes(1, cg, (nc.sync, nc.sync))
+        def gather_words(name, table):
+            gathered = keep.tile([P, SLOTS], U32, name=name, tag=name, align_bytes=64)
+            nc.vector.tensor_copy(gathered[:], table[:].indirect(offsets[:]))
+            return gathered
 
-        def gather_words(name, win):
-            g = keep.tile([P, SLOTS], U32, name=name + "_g", align_bytes=64)
-            nc.vector.tensor_copy(g[:], win[:].indirect(offsets[:]))
-            src = g[:].bitcast(U16).rearrange("p (c i r h) -> p h c r i", h=PASSES, r=PACK, i=4)
-            pairs = []
-            for u in range(2):
-                w = keep.tile([P, PASSES * 2 * P * 2], U8, name="%s_w%d" % (name, u), align_bytes=64)
-                nc.vector.tensor_copy(
-                    w[:].bitcast(U16).rearrange("p (h r c i) -> p h c r i", h=PASSES, r=2, i=4),
-                    src[:, :, :, 2 * u : 2 * u + 2, :],
-                )
-                pairs.append(w)
-            return pairs
+        def split_words(name, gathered):
+            halves = gathered[:].bitcast(U16).rearrange("p (m r o) -> p r m o", r=PACK, o=PASSES)
+            tiles = []
+            for r in range(PACK):
+                words = keep.tile([P, PASSES * P * 2], U8, name="%s%d" % (name, r), align_bytes=64)
+                nc.vector.tensor_copy(words[:].bitcast(U16).rearrange("p (o m) -> p m o", o=PASSES), halves[:, r])
+                tiles.append(words)
+            return tiles
 
-        qcodes = keep.tile([P, PASSES, NQ], U32, name="qcodes", align_bytes=64)
-        qscales = keep.tile([P, PASSES, NQ], U8, name="qscales", align_bytes=64)
-        ycodes = keep.tile([P, NQ], U32, name="ycodes", align_bytes=64)
-        yscales = keep.tile([P, NQ], U8, name="yscales", align_bytes=64)
-        S, V = nc.scalar.copy, nc.vector.tensor_copy
+        q_raw0 = load_q(0, "q_raw0")
+        k_table = load_words("k_words", k_words, "k_words")
+        fill_planes(GATE, gather_scales(GATE), "scales_dealt0")
+        q_raw1 = load_q(1, "scales_gathered0")
+        c_scales_gathered = gather_scales(LAYER)
+        c_table = load_words("c_words", c_words, "c_scales")
+
+        q_codes = keep.tile([P, PASSES, NQ], U32, name="q_codes", align_bytes=64)
+        q_scales = keep.tile([P, PASSES, NQ], U8, name="q_scales", align_bytes=64)
+        y_codes = keep.tile([P, NQ], U32, name="y_codes", align_bytes=64)
+        y_scales = keep.tile([P, NQ], U8, name="y_scales", align_bytes=64)
 
         def quantise_q(o, raw):
-            qb = keep.tile([P, NQ, PACK], BF16, name="qb%d" % o, align_bytes=64)
-            halves = (slice(0, NQ // 2), slice(NQ // 2, NQ))
-            interleave(S, qb[:, halves[1], :], raw[:, :, halves[1]])
-            interleave(V, qb[:, halves[0], :], raw[:, :, halves[0]])
-            for cols in halves:
+            grouped = keep.tile([P, NQ, PACK], BF16, name="q_grouped%d" % o, align_bytes=64)
+            low, high = slice(0, NQ // 2), slice(NQ // 2, NQ)
+            interleave(nc.scalar.copy, grouped[:, high, :], raw[:, :, high])
+            interleave(nc.vector.tensor_copy, grouped[:, low, :], raw[:, :, low])
+            for cols in (low, high):
                 nc.vector.quantize_mx(
-                    out=qcodes[:, o, cols].bitcast(FP8X4),
-                    scales=qscales[:, o, cols],
-                    in_=qb[:, cols, :].rearrange("p n t -> p (n t)"),
+                    out=q_codes[:, o, cols].bitcast(FP8X4),
+                    scales=q_scales[:, o, cols],
+                    in_=grouped[:, cols, :].rearrange("p n t -> p (n t)"),
                 )
 
-        def one_pass(acc, pairs, w, r, o):
-            col = (o * 2 + r % 2) * P
+        def one_pass(acc, words, w, r, o):
             nc.tensor.matmul_mx(
                 out=acc[:],
-                lhsT=pairs[r // 2][:, 2 * col : 2 * (col + P)].bitcast(FP4X4),
+                lhsT=words[r][:, 2 * o * P : 2 * (o + 1) * P].bitcast(FP4X4),
                 lhsT_scale=planes[w][:, o, r * P : (r + 1) * P],
-                rhs=qcodes[:, o, :].bitcast(FP8X4),
-                rhs_scale=qscales[:, o, :],
+                rhs=q_codes[:, o, :].bitcast(FP8X4),
+                rhs_scale=q_scales[:, o, :],
                 start=(o == 0),
                 stop=(o == PASSES - 1),
             )
 
-        quantise_q(0, qraw0)
-        kpairs = gather_words("k", kw)
+        quantise_q(0, q_raw0)
+        k_gathered = gather_words("k_gathered", k_table)
+        k_split = split_words("k_split", k_gathered)
+        fill_planes(LAYER, c_scales_gathered, "k_gathered")
         a = [psum.tile([P, NQ], F32, name="a%d" % r) for r in range(PACK)]
         for r in range(PACK):
-            one_pass(a[r], kpairs, 0, r, 0)
-        quantise_q(1, qraw1)
-        s = keep.tile([P, PACK, NQ], F32, name="s")
+            one_pass(a[r], k_split, GATE, r, 0)
+        quantise_q(1, q_raw1)
+        gate = keep.tile([P, PACK, NQ], F32, name="gate")
         for r in range(PACK):
-            one_pass(a[r], kpairs, 0, r, 1)
-            nc.scalar.activation(s[:, r, :], a[r][:], SILU)
+            one_pass(a[r], k_split, GATE, r, 1)
+            nc.scalar.activation(gate[:, r, :], a[r][:], SILU)
 
-        cpairs = gather_words("c", cw)
+        c_split = split_words("c_split", gather_words("c_gathered", c_table))
         y = keep.tile([P, PACK, NQ], F32, name="y")
-        yb = keep.tile([P, NQ, PACK], BF16, name="yb", align_bytes=64)
+        y_grouped = keep.tile([P, NQ, PACK], BF16, name="y_grouped", align_bytes=64)
         out_rows = out_0.rearrange("(p r) n -> p r n", r=PACK)
-        first, second, rest = slice(0, CH), slice(CH, 2 * CH), slice(2 * CH, NQ)
+        quarter0, quarter1, last_half = slice(0, NQ // 4), slice(NQ // 4, NQ // 2), slice(NQ // 2, NQ)
         for r in range(PACK):
             z = psum.tile([P, NQ], F32, name="z%d" % r)
             for o in range(PASSES):
-                one_pass(z, cpairs, 1, r, o)
-            for cols in (slice(0, NQ),) if r < PACK - 1 else (first, rest, second):
-                nc.vector.tensor_tensor(y[:, r, cols], z[:, cols], s[:, r, cols], MULT)
+                one_pass(z, c_split, LAYER, r, o)
+            for cols in (slice(0, NQ),) if r < PACK - 1 else (quarter0, last_half, quarter1):
+                nc.vector.tensor_tensor(y[:, r, cols], z[:, cols], gate[:, r, cols], MULT)
             nc.sync.dma_start(out_rows[:, r, :], y[:, r, :])
 
         def quantise_y(cols):
             nc.vector.quantize_mx(
-                out=ycodes[:, cols].bitcast(FP8X4),
-                scales=yscales[:, cols],
-                in_=yb[:, cols, :].rearrange("p n t -> p (n t)"),
+                out=y_codes[:, cols].bitcast(FP8X4),
+                scales=y_scales[:, cols],
+                in_=y_grouped[:, cols, :].rearrange("p n t -> p (n t)"),
             )
 
         def store_codes(cols):
             nc.sync.dma_start(
-                out_1[0, :, cols, :].rearrange("p n b -> p (n b)").bitcast(I32), ycodes[:, cols].bitcast(I32)
+                out_1[0, :, cols, :].rearrange("p n b -> p (n b)").bitcast(I32), y_codes[:, cols].bitcast(I32)
             )
 
-        interleave(S, yb[:, first, :], y[:, :, first])
-        interleave(S, yb[:, second, :], y[:, :, second])
-        interleave(V, yb[:, rest, :], y[:, :, rest])
-        quantise_y(first)
-        quantise_y(rest)
-        store_codes(rest)
-        quantise_y(second)
-        store_codes(slice(0, 2 * CH))
-        for Q in range(4):
-            nc.scalar.dma_start(
-                out_2[0, 4 * Q : 4 * Q + 4, :].bitcast(I32), yscales[32 * Q : 32 * Q + 4, :].bitcast(I32)
+        interleave(nc.scalar.copy, y_grouped[:, quarter0, :], y[:, :, quarter0])
+        interleave(nc.scalar.copy, y_grouped[:, quarter1, :], y[:, :, quarter1])
+        interleave(nc.vector.tensor_copy, y_grouped[:, last_half, :], y[:, :, last_half])
+        quantise_y(quarter0)
+        quantise_y(last_half)
+        store_codes(last_half)
+        quantise_y(quarter1)
+        store_codes(slice(0, NQ // 2))
+        for quad in range(QUADS):
+            queue = nc.sync if quad == QUADS - 1 else nc.scalar
+            queue.dma_start(
+                out_2[0, 4 * quad : 4 * quad + 4, :].bitcast(I32), y_scales[32 * quad : 32 * quad + 4, :].bitcast(I32)
             )

@@ -90,12 +90,14 @@ def tile_attend_plh_swiglu4_topk_kernel(tc, qT, k_words, k_scales, c_words, c_sc
             nc.vector.tensor_copy(gathered[:], table[:].indirect(offsets[:]))
             return gathered
 
-        def split_words(name, gathered):
+        def split_words(name, gathered, first_in_halves=False):
             halves = gathered[:].bitcast(U16).rearrange("p (m r o) -> p r m o", r=PACK, o=PASSES)
             tiles = []
             for r in range(PACK):
                 words = keep.tile([P, PASSES * P * 2], U8, name="%s%d" % (name, r), align_bytes=64)
-                nc.vector.tensor_copy(words[:].bitcast(U16).rearrange("p (o m) -> p m o", o=PASSES), halves[:, r])
+                by_slot = words[:].bitcast(U16).rearrange("p (o m) -> p m o", o=PASSES)
+                for m in (slice(0, P // 2), slice(P // 2, P)) if first_in_halves and r == 0 else (slice(0, P),):
+                    nc.vector.tensor_copy(by_slot[:, m, :], halves[:, r, m, :])
                 tiles.append(words)
             return tiles
 
@@ -147,16 +149,21 @@ def tile_attend_plh_swiglu4_topk_kernel(tc, qT, k_words, k_scales, c_words, c_sc
             one_pass(a[r], k_split, GATE, r, 1)
             nc.scalar.activation(gate[:, r, :], a[r][:], SILU)
 
-        c_split = split_words("c_split", gather_words("c_gathered", c_table))
+        c_gathered = keep.tile([P, SLOTS], U32, name="c_gathered", align_bytes=64)
+        for half in range(2):
+            slots = slice(half * SLOTS // 2, (half + 1) * SLOTS // 2)
+            entries = offsets[:, slots.start // 16 : slots.stop // 16]
+            nc.vector.tensor_copy(c_gathered[:, slots], c_table[:].indirect(entries))
+        c_split = split_words("c_split", c_gathered, first_in_halves=True)
         y = keep.tile([P, PACK, NQ], F32, name="y")
         y_grouped = keep.tile([P, NQ, PACK], BF16, name="y_grouped", align_bytes=64)
         out_rows = out_0.rearrange("(p r) n -> p r n", r=PACK)
-        quarter0, quarter1, last_half = slice(0, NQ // 4), slice(NQ // 4, NQ // 2), slice(NQ // 2, NQ)
+        first, middle, last = slice(0, NQ // 4), slice(NQ // 4, 3 * NQ // 4), slice(3 * NQ // 4, NQ)
         for r in range(PACK):
             z = psum.tile([P, NQ], F32, name="z%d" % r)
             for o in range(PASSES):
                 one_pass(z, c_split, LAYER, r, o)
-            for cols in (slice(0, NQ),) if r < PACK - 1 else (quarter0, last_half, quarter1):
+            for cols in (slice(0, NQ),) if r < PACK - 1 else (first, middle, last):
                 nc.vector.tensor_tensor(y[:, r, cols], z[:, cols], gate[:, r, cols], MULT)
             nc.sync.dma_start(out_rows[:, r, :], y[:, r, :])
 
@@ -172,16 +179,16 @@ def tile_attend_plh_swiglu4_topk_kernel(tc, qT, k_words, k_scales, c_words, c_sc
                 out_1[0, :, cols, :].rearrange("p n b -> p (n b)").bitcast(I32), y_codes[:, cols].bitcast(I32)
             )
 
-        interleave(nc.scalar.copy, y_grouped[:, quarter0, :], y[:, :, quarter0])
-        interleave(nc.scalar.copy, y_grouped[:, quarter1, :], y[:, :, quarter1])
-        interleave(nc.vector.tensor_copy, y_grouped[:, last_half, :], y[:, :, last_half])
-        quantise_y(quarter0)
-        quantise_y(last_half)
-        store_codes(last_half)
-        quantise_y(quarter1)
-        store_codes(slice(0, NQ // 2))
+        interleave(nc.scalar.copy, y_grouped[:, first, :], y[:, :, first])
+        interleave(nc.scalar.copy, y_grouped[:, last, :], y[:, :, last])
+        interleave(nc.vector.tensor_copy, y_grouped[:, middle, :], y[:, :, middle])
+        quantise_y(first)
+        quantise_y(middle)
+        store_codes(slice(first.start, middle.stop))
+        quantise_y(last)
+        store_codes(last)
         for quad in range(QUADS):
-            queue = nc.sync if quad == QUADS - 1 else nc.scalar
+            queue = nc.sync if quad >= QUADS // 2 else nc.scalar
             queue.dma_start(
                 out_2[0, 4 * quad : 4 * quad + 4, :].bitcast(I32), y_scales[32 * quad : 32 * quad + 4, :].bitcast(I32)
             )

@@ -23,6 +23,9 @@ PASSES = D // K_PASS
 QUADS = 4
 SCALE_ROW0 = P - 32
 GATE, LAYER = 0, 1
+HALF = NQ // 2
+EARLY, LATE = 0, 1
+PAIRS = 2
 
 
 def interleave(copy, dst, src):
@@ -37,14 +40,21 @@ def tile_attend_plh_swiglu4_topk_kernel(tc, qT, k_words, k_scales, c_words, c_sc
     with ExitStack() as ctx:
         lists = ctx.enter_context(tc.tile_pool(name="lists", bufs=1))
         keep = ctx.enter_context(tc.tile_pool(name="keep", bufs=1))
+        placed = ctx.enter_context(tc.tile_pool(name="placed", bufs=1))
+        late_steps = ctx.enter_context(tc.tile_pool(name="late_steps", bufs=1))
         psum = ctx.enter_context(tc.psum_pool(name="psum", bufs=1))
 
         offsets = lists.tile([P, SLOTS // 16], U16, name="offsets")
         nc.sync.dma_start(offsets[:], offs)
 
+        warm = keep.tile([P, 2], F32, name="warm")
+        nc.gpsimd.memset(warm[:, 0:1], 0.0)
+        nc.scalar.activation(warm[:, 1:2], warm[:, 0:1], SILU)
+
         scale_tables = []
         for name, scales in (("k_scales", k_scales), ("c_scales", c_scales)):
-            table = keep.tile([P, NEURONS], U8, name=name, tag=name, align_bytes=64)
+            at = 2 * PACK * HALF * 4 - NEURONS // 2 if name == "k_scales" else 0
+            table = placed.tile([P, NEURONS], U8, name=name, align_bytes=64, offset=at)
             nc.sync.dma_start(table[SCALE_ROW0:P, :].bitcast(I32), scales.rearrange("o f t -> f o t").bitcast(I32))
             nc.vector.memset(table[0:SCALE_ROW0, :].bitcast(I32), 0)
             scale_tables.append(table)
@@ -55,29 +65,24 @@ def tile_attend_plh_swiglu4_topk_kernel(tc, qT, k_words, k_scales, c_words, c_sc
             nc.vector.memset(plane[:].rearrange("p o s -> p (o s)").bitcast(I32), 0)
             planes.append(plane)
 
-        def load_words(name, words, tag):
-            table = keep.tile([P, NEURONS], U32, name=name, tag=tag, align_bytes=64)
+        def load_words(table, words):
             nc.sync.dma_start(table[:].bitcast(I32), words[0].rearrange("p t b -> p (t b)").bitcast(I32))
-            return table
 
-        def load_q(o, tag):
-            raw = keep.tile([P, PACK, NQ], F32, name="q_raw%d" % o, tag=tag, align_bytes=64)
-            rows = qT[0, K_PASS * o : K_PASS * (o + 1), :]
+        def load_q(raw, h, o):
+            rows = qT[0, K_PASS * o : K_PASS * (o + 1), HALF * h : HALF * (h + 1)]
             nc.sync.dma_start(raw[:], rows.rearrange("(p j) n -> p j n", j=PACK))
-            return raw
 
         def gather_scales(w):
-            name = "scales_gathered%d" % w
-            gathered = keep.tile([P, SLOTS], U8, name=name, tag=name, align_bytes=64)
-            nc.vector.tensor_copy(gathered[:], scale_tables[w][:].indirect(offsets[:]))
-            return gathered
-
-        def fill_planes(w, gathered, tag):
-            dealt = keep.tile([P, SLOTS], U8, name="scales_dealt%d" % w, tag=tag, align_bytes=64)
+            if w == GATE:
+                dealt = keep.tile([P, SLOTS], U8, name="k_scales_dealt", align_bytes=64)
+            else:
+                dealt = late_steps.tile([P, SLOTS], U8, name="c_scales_dealt", align_bytes=64, offset=960)
             nc.vector.tensor_copy(
-                dealt[:].rearrange("p (r c i) -> p c r i", r=PACK, i=16),
-                gathered[:].rearrange("p (c i r) -> p c r i", r=PACK, i=16),
+                dealt[:].rearrange("p (r m) -> p m r", r=PACK), scale_tables[w][:].indirect(offsets[:])
             )
+            return dealt
+
+        def move_scales(w, dealt):
             for quad in range(QUADS):
                 first_row = SCALE_ROW0 + 8 * quad
                 nc.sync.dma_start(
@@ -86,107 +91,172 @@ def tile_attend_plh_swiglu4_topk_kernel(tc, qT, k_words, k_scales, c_words, c_sc
                 )
 
         def gather_words(name, table):
-            gathered = keep.tile([P, SLOTS], U32, name=name, tag=name, align_bytes=64)
+            gathered = keep.tile([P, SLOTS], U32, name=name, align_bytes=64)
             nc.vector.tensor_copy(gathered[:], table[:].indirect(offsets[:]))
             return gathered
 
-        def split_words(name, gathered, first_in_halves=False):
+        def gather_words_in_halves(name, table):
+            gathered = keep.tile([P, SLOTS], U32, name=name, align_bytes=64)
+            for half in range(2):
+                slots = slice(half * SLOTS // 2, (half + 1) * SLOTS // 2)
+                entries = offsets[:, slots.start // 16 : slots.stop // 16]
+                nc.vector.tensor_copy(gathered[:, slots], table[:].indirect(entries))
+            return gathered
+
+        def split_words(words, gathered, pair, in_halves=False):
             halves = gathered[:].bitcast(U16).rearrange("p (m r o) -> p r m o", r=PACK, o=PASSES)
-            tiles = []
-            for r in range(PACK):
-                words = keep.tile([P, PASSES * P * 2], U8, name="%s%d" % (name, r), align_bytes=64)
-                by_slot = words[:].bitcast(U16).rearrange("p (o m) -> p m o", o=PASSES)
-                for m in (slice(0, P // 2), slice(P // 2, P)) if first_in_halves and r == 0 else (slice(0, P),):
-                    nc.vector.tensor_copy(by_slot[:, m, :], halves[:, r, m, :])
-                tiles.append(words)
-            return tiles
+            by_slot = words[:].bitcast(U16).rearrange("p (r o m) -> p r m o", r=2, o=PASSES)
+            for m in (slice(0, P // 2), slice(P // 2, P)) if in_halves else (slice(0, P),):
+                nc.vector.tensor_copy(by_slot[:, :, m, :], halves[:, 2 * pair : 2 * pair + 2, m, :])
 
-        q_raw0 = load_q(0, "q_raw0")
-        k_table = load_words("k_words", k_words, "k_words")
-        fill_planes(GATE, gather_scales(GATE), "scales_dealt0")
-        q_raw1 = load_q(1, "scales_gathered0")
-        c_scales_gathered = gather_scales(LAYER)
-        c_table = load_words("c_words", c_words, "c_scales")
+        split_bytes = 2 * PASSES * P * 2
 
-        q_codes = keep.tile([P, PASSES, NQ], U32, name="q_codes", align_bytes=64)
-        q_scales = keep.tile([P, PASSES, NQ], U8, name="q_scales", align_bytes=64)
+        raw_bytes = PACK * HALF * 4
+        k_table = keep.tile([P, NEURONS], U32, name="k_table", align_bytes=64)
+        load_words(k_table, k_words)
+        raw0 = keep.tile([P, PACK, NQ], F32, name="q_raw0", align_bytes=64)
+        nc.sync.dma_start(raw0[:], qT[0, 0:K_PASS, :].rearrange("(p j) n -> p j n", j=PACK))
+        raw = {(h, 0): raw0[:, :, HALF * h : HALF * (h + 1)] for h in (EARLY, LATE)}
+        move_scales(GATE, gather_scales(GATE))
+        early = placed.tile([P, PACK, HALF], F32, name="q_raw10", align_bytes=64, offset=raw_bytes)
+        c_table = placed.tile([P, NEURONS], U32, name="c_table", align_bytes=64, offset=2 * raw_bytes)
+        load_words(c_table, c_words)
+        load_q(early, EARLY, 1)
+        move_scales(LAYER, gather_scales(LAYER))
+        late = placed.tile([P, PACK, HALF], F32, name="q_raw11", align_bytes=64, offset=0)
+        load_q(late, LATE, 1)
+        raw[EARLY, 1], raw[LATE, 1] = early[:], late[:]
+
+        q_codes, q_scales, grouped = {}, {}, {}
+        for h in (EARLY, LATE):
+            for o in range(PASSES):
+                name = "q_grouped%d%d" % (h, o)
+                grouped[h, o] = keep.tile([P, HALF, PACK], BF16, name=name, tag=name, align_bytes=64)
+        for h in (EARLY, LATE):
+            for o in range(PASSES):
+                name = "q_codes%d%d" % (h, o)
+                q_codes[h, o] = keep.tile([P, HALF], U32, name=name, align_bytes=64)
+                if (h, o) == (EARLY, 1):
+                    q_scales[h, o] = late_steps.tile([P, HALF], U8, name="q_scales01", align_bytes=64, offset=1024)
+                else:
+                    q_scales[h, o] = keep.tile([P, HALF], U8, name="q_scales%d%d" % (h, o), align_bytes=64)
         y_codes = keep.tile([P, NQ], U32, name="y_codes", align_bytes=64)
         y_scales = keep.tile([P, NQ], U8, name="y_scales", align_bytes=64)
+        low, high, both = slice(0, HALF // 2), slice(HALF // 2, HALF), slice(0, HALF)
 
-        def quantise_q(o, raw):
-            grouped = keep.tile([P, NQ, PACK], BF16, name="q_grouped%d" % o, align_bytes=64)
-            low, high = slice(0, NQ // 2), slice(NQ // 2, NQ)
-            interleave(nc.scalar.copy, grouped[:, high, :], raw[:, :, high])
-            interleave(nc.vector.tensor_copy, grouped[:, low, :], raw[:, :, low])
-            for cols in (low, high):
-                nc.vector.quantize_mx(
-                    out=q_codes[:, o, cols].bitcast(FP8X4),
-                    scales=q_scales[:, o, cols],
-                    in_=grouped[:, cols, :].rearrange("p n t -> p (n t)"),
+        def round_q(copy, h, o, cols):
+            interleave(copy, grouped[h, o][:, cols, :], raw[h, o][:, :, cols])
+
+        def quantise_q(h, o, cols):
+            nc.vector.quantize_mx(
+                out=q_codes[h, o][:, cols].bitcast(FP8X4),
+                scales=q_scales[h, o][:, cols],
+                in_=grouped[h, o][:, cols, :].rearrange("p n t -> p (n t)"),
+            )
+
+        banks = {}
+        for h in (EARLY, LATE):
+            for w in (GATE, LAYER):
+                for pair in range(PAIRS):
+                    tag = "bank%d%d%d" % (w, h, pair)
+                    banks[w, h, pair] = psum.tile([P, 2, HALF], F32, name="bank%d%d%d" % (w, h, pair), tag=tag)
+
+        def bank_pass(words, w, h, pair, o, opening=0):
+            for i in range(2):
+                r = 2 * pair + i
+                first = 2 * P * (PASSES * i + o)
+                nc.tensor.matmul_mx(
+                    out=banks[w, h, pair][:, i, :],
+                    lhsT=words[pair][:, first : first + 2 * P].bitcast(FP4X4),
+                    lhsT_scale=planes[w][:, o, r * P : (r + 1) * P],
+                    rhs=q_codes[h, o][:].bitcast(FP8X4),
+                    rhs_scale=q_scales[h, o][:],
+                    start=(o == opening and i == 0),
+                    stop=(o != opening and i == 1),
                 )
 
-        def one_pass(acc, words, w, r, o):
-            nc.tensor.matmul_mx(
-                out=acc[:],
-                lhsT=words[r][:, 2 * o * P : 2 * (o + 1) * P].bitcast(FP4X4),
-                lhsT_scale=planes[w][:, o, r * P : (r + 1) * P],
-                rhs=q_codes[:, o, :].bitcast(FP8X4),
-                rhs_scale=q_scales[:, o, :],
-                start=(o == 0),
-                stop=(o == PASSES - 1),
-            )
-
-        quantise_q(0, q_raw0)
-        k_gathered = gather_words("k_gathered", k_table)
-        k_split = split_words("k_split", k_gathered)
-        fill_planes(LAYER, c_scales_gathered, "k_gathered")
-        a = [psum.tile([P, NQ], F32, name="a%d" % r) for r in range(PACK)]
-        for r in range(PACK):
-            one_pass(a[r], k_split, GATE, r, 0)
-        quantise_q(1, q_raw1)
-        gate = keep.tile([P, PACK, NQ], F32, name="gate")
-        for r in range(PACK):
-            one_pass(a[r], k_split, GATE, r, 1)
-            nc.scalar.activation(gate[:, r, :], a[r][:], SILU)
-
-        c_gathered = keep.tile([P, SLOTS], U32, name="c_gathered", align_bytes=64)
-        for half in range(2):
-            slots = slice(half * SLOTS // 2, (half + 1) * SLOTS // 2)
-            entries = offsets[:, slots.start // 16 : slots.stop // 16]
-            nc.vector.tensor_copy(c_gathered[:, slots], c_table[:].indirect(entries))
-        c_split = split_words("c_split", c_gathered, first_in_halves=True)
-        y = keep.tile([P, PACK, NQ], F32, name="y")
-        y_grouped = keep.tile([P, NQ, PACK], BF16, name="y_grouped", align_bytes=64)
+        gate, y, y_grouped = {}, {}, {}
+        for h in (EARLY, LATE):
+            gate[h] = keep.tile([P, PACK, HALF], F32, name="gate%d" % h)
+            y_grouped[h] = keep.tile([P, HALF, PACK], BF16, name="y_grouped%d" % h, align_bytes=64)
+            if h == EARLY:
+                y[h] = placed.tile([P, PACK, HALF], F32, name="y0", align_bytes=64, offset=0)
+            else:
+                y[h] = keep.tile([P, PACK, HALF], F32, name="y1")
         out_rows = out_0.rearrange("(p r) n -> p r n", r=PACK)
-        first, middle, last = slice(0, NQ // 4), slice(NQ // 4, 3 * NQ // 4), slice(3 * NQ // 4, NQ)
-        for r in range(PACK):
-            z = psum.tile([P, NQ], F32, name="z%d" % r)
-            for o in range(PASSES):
-                one_pass(z, c_split, LAYER, r, o)
-            for cols in (slice(0, NQ),) if r < PACK - 1 else (first, middle, last):
-                nc.vector.tensor_tensor(y[:, r, cols], z[:, cols], gate[:, r, cols], MULT)
-            nc.sync.dma_start(out_rows[:, r, :], y[:, r, :])
 
-        def quantise_y(cols):
+        def silu(h, pair):
+            nc.scalar.activation(gate[h][:, 2 * pair : 2 * pair + 2, :], banks[GATE, h, pair][:], SILU)
+
+        def product(h, pair):
+            rows = slice(2 * pair, 2 * pair + 2)
+            nc.vector.tensor_tensor(y[h][:, rows, :], banks[LAYER, h, pair][:], gate[h][:, rows, :], MULT)
+            nc.sync.dma_start(out_rows[:, rows, HALF * h : HALF * (h + 1)], y[h][:, rows, :])
+
+        def round_y(copy, h, cols):
+            interleave(copy, y_grouped[h][:, cols, :], y[h][:, :, cols])
+
+        def quantise_y(h, cols):
+            at = slice(HALF * h + cols.start, HALF * h + cols.stop)
             nc.vector.quantize_mx(
-                out=y_codes[:, cols].bitcast(FP8X4),
-                scales=y_scales[:, cols],
-                in_=y_grouped[:, cols, :].rearrange("p n t -> p (n t)"),
+                out=y_codes[:, at].bitcast(FP8X4),
+                scales=y_scales[:, at],
+                in_=y_grouped[h][:, cols, :].rearrange("p n t -> p (n t)"),
             )
 
-        def store_codes(cols):
+        def store_codes(h):
+            at = slice(HALF * h, HALF * (h + 1))
             nc.sync.dma_start(
-                out_1[0, :, cols, :].rearrange("p n b -> p (n b)").bitcast(I32), y_codes[:, cols].bitcast(I32)
+                out_1[0, :, at, :].rearrange("p n b -> p (n b)").bitcast(I32), y_codes[:, at].bitcast(I32)
             )
 
-        interleave(nc.scalar.copy, y_grouped[:, first, :], y[:, :, first])
-        interleave(nc.scalar.copy, y_grouped[:, last, :], y[:, :, last])
-        interleave(nc.vector.tensor_copy, y_grouped[:, middle, :], y[:, :, middle])
-        quantise_y(first)
-        quantise_y(middle)
-        store_codes(slice(first.start, middle.stop))
-        quantise_y(last)
-        store_codes(last)
+        k_gathered = gather_words("k_gathered", k_table)
+        k_split = [keep.tile([P, split_bytes], U8, name="k_split%d" % pair, align_bytes=64) for pair in range(PAIRS)]
+        for pair in range(PAIRS):
+            split_words(k_split[pair], k_gathered, pair)
+        round_q(nc.vector.tensor_copy, LATE, 0, both)
+        round_q(nc.scalar.copy, EARLY, 0, both)
+        for h in (LATE, EARLY):
+            quantise_q(h, 0, both)
+            for pair in range(PAIRS):
+                bank_pass(k_split, GATE, h, pair, 0)
+        c_gathered = gather_words("c_gathered", c_table)
+        c_split = [
+            late_steps.tile([P, split_bytes], U8, name="c_split%d" % pair, align_bytes=64, offset=1280 * pair)
+            for pair in range(PAIRS)
+        ]
+        round_q(nc.scalar.copy, EARLY, 1, low)
+        round_q(nc.vector.tensor_copy, EARLY, 1, high)
+        split_words(c_split[0], c_gathered, 0)
+        bank_pass(c_split, LAYER, EARLY, 0, 0)
+        quantise_q(EARLY, 1, both)
+        split_words(c_split[1], c_gathered, 1)
+        for pair in range(PAIRS):
+            bank_pass(k_split, GATE, EARLY, pair, 1)
+            silu(EARLY, pair)
+        bank_pass(c_split, LAYER, EARLY, 0, 1)
+        for o in range(PASSES):
+            bank_pass(c_split, LAYER, EARLY, 1, o)
+        for cols in (low, high):
+            round_q(nc.vector.tensor_copy, LATE, 1, cols)
+        for cols in (low, high):
+            quantise_q(LATE, 1, cols)
+        for pair in range(PAIRS):
+            bank_pass(k_split, GATE, LATE, pair, 1)
+            silu(LATE, pair)
+        product(EARLY, 0)
+        product(EARLY, 1)
+        for pair in range(PAIRS):
+            for o in (1, 0):
+                bank_pass(c_split, LAYER, LATE, pair, o, opening=1)
+            product(LATE, pair)
+        round_y(nc.scalar.copy, EARLY, both)
+        round_y(nc.scalar.copy, LATE, slice(192, HALF))
+        round_y(nc.vector.tensor_copy, LATE, slice(0, 192))
+        quantise_y(EARLY, both)
+        store_codes(EARLY)
+        quantise_y(LATE, both)
+        store_codes(LATE)
         for quad in range(QUADS):
             queue = nc.sync if quad >= QUADS // 2 else nc.scalar
             queue.dma_start(

@@ -95,19 +95,10 @@ def tile_attend_plh_swiglu4_topk_kernel(tc, qT, k_words, k_scales, c_words, c_sc
             nc.vector.tensor_copy(gathered[:], table[:].indirect(offsets[:]))
             return gathered
 
-        def gather_words_in_halves(name, table):
-            gathered = keep.tile([P, SLOTS], U32, name=name, align_bytes=64)
-            for half in range(2):
-                slots = slice(half * SLOTS // 2, (half + 1) * SLOTS // 2)
-                entries = offsets[:, slots.start // 16 : slots.stop // 16]
-                nc.vector.tensor_copy(gathered[:, slots], table[:].indirect(entries))
-            return gathered
-
-        def split_words(words, gathered, pair, in_halves=False):
-            halves = gathered[:].bitcast(U16).rearrange("p (m r o) -> p r m o", r=PACK, o=PASSES)
-            by_slot = words[:].bitcast(U16).rearrange("p (r o m) -> p r m o", r=2, o=PASSES)
-            for m in (slice(0, P // 2), slice(P // 2, P)) if in_halves else (slice(0, P),):
-                nc.vector.tensor_copy(by_slot[:, :, m, :], halves[:, 2 * pair : 2 * pair + 2, m, :])
+        def split_words(words, gathered, pair):
+            halves = gathered[:].bitcast(U16).rearrange("p (m r o) -> p m r o", r=PACK, o=PASSES)
+            by_slot = words[:].bitcast(U16).rearrange("p (r o m) -> p m r o", r=2, o=PASSES)
+            nc.vector.tensor_copy(by_slot, halves[:, :, 2 * pair : 2 * pair + 2, :])
 
         split_bytes = 2 * PASSES * P * 2
 

@@ -95,10 +95,19 @@ def tile_attend_plh_swiglu4_topk_kernel(tc, qT, k_words, k_scales, c_words, c_sc
             nc.vector.tensor_copy(gathered[:], table[:].indirect(offsets[:]))
             return gathered
 
-        def split_words(words, gathered, pair):
+        def gather_words_in_halves(name, table):
+            gathered = keep.tile([P, SLOTS], U32, name=name, align_bytes=64)
+            for half in range(2):
+                slots = slice(half * SLOTS // 2, (half + 1) * SLOTS // 2)
+                entries = offsets[:, slots.start // 16 : slots.stop // 16]
+                nc.vector.tensor_copy(gathered[:, slots], table[:].indirect(entries))
+            return gathered
+
+        def split_words(words, gathered, pair, pieces=(slice(0, P),)):
             halves = gathered[:].bitcast(U16).rearrange("p (m r o) -> p m r o", r=PACK, o=PASSES)
             by_slot = words[:].bitcast(U16).rearrange("p (r o m) -> p m r o", r=2, o=PASSES)
-            nc.vector.tensor_copy(by_slot, halves[:, :, 2 * pair : 2 * pair + 2, :])
+            for m in pieces:
+                nc.vector.tensor_copy(by_slot[:, m], halves[:, m, 2 * pair : 2 * pair + 2, :])
 
         split_bytes = 2 * PASSES * P * 2
 
@@ -211,17 +220,18 @@ def tile_attend_plh_swiglu4_topk_kernel(tc, qT, k_words, k_scales, c_words, c_sc
             quantise_q(h, 0, both)
             for pair in range(PAIRS):
                 bank_pass(k_split, GATE, h, pair, 0)
-        c_gathered = gather_words("c_gathered", c_table)
+        c_gathered = gather_words_in_halves("c_gathered", c_table)
         c_split = [
-            late_steps.tile([P, split_bytes], U8, name="c_split%d" % pair, align_bytes=64, offset=1280 * pair)
-            for pair in range(PAIRS)
+            keep.tile([P, split_bytes], U8, name="c_split0", align_bytes=64),
+            late_steps.tile([P, split_bytes], U8, name="c_split1", align_bytes=64, offset=1280),
         ]
+        split_words(c_split[0], c_gathered, 0, (slice(0, P // 2), slice(P // 2, P)))
         round_q(nc.scalar.copy, EARLY, 1, low)
         round_q(nc.vector.tensor_copy, EARLY, 1, high)
-        split_words(c_split[0], c_gathered, 0)
-        bank_pass(c_split, LAYER, EARLY, 0, 0)
-        quantise_q(EARLY, 1, both)
+        for h in (EARLY, LATE):
+            bank_pass(c_split, LAYER, h, 0, 0)
         split_words(c_split[1], c_gathered, 1)
+        quantise_q(EARLY, 1, both)
         for pair in range(PAIRS):
             bank_pass(k_split, GATE, EARLY, pair, 1)
             silu(EARLY, pair)
@@ -238,8 +248,8 @@ def tile_attend_plh_swiglu4_topk_kernel(tc, qT, k_words, k_scales, c_words, c_sc
         product(EARLY, 0)
         product(EARLY, 1)
         for pair in range(PAIRS):
-            for o in (1, 0):
-                bank_pass(c_split, LAYER, LATE, pair, o, opening=1)
+            for o in (1,) if pair == 0 else (1, 0):
+                bank_pass(c_split, LAYER, LATE, pair, o, opening=pair)
             product(LATE, pair)
         round_y(nc.scalar.copy, EARLY, both)
         round_y(nc.scalar.copy, LATE, slice(192, HALF))

@@ -56,7 +56,7 @@ def tile_attend_plh_swiglu4_topk_kernel(tc, qT, k_words, k_scales, c_words, c_sc
             at = 2 * PACK * HALF * 4 - NEURONS // 2 if name == "k_scales" else 0
             table = placed.tile([P, NEURONS], U8, name=name, align_bytes=64, offset=at)
             nc.sync.dma_start(table[SCALE_ROW0:P, :].bitcast(I32), scales.rearrange("o f t -> f o t").bitcast(I32))
-            nc.vector.memset(table[0:SCALE_ROW0, :].bitcast(I32), 0)
+            nc.gpsimd.memset(table[0:SCALE_ROW0, :].bitcast(I32), 0)
             scale_tables.append(table)
 
         planes = []
@@ -89,11 +89,6 @@ def tile_attend_plh_swiglu4_topk_kernel(tc, qT, k_words, k_scales, c_words, c_sc
                     planes[w][32 * quad : 32 * quad + 4].bitcast(I32),
                     dealt[first_row : first_row + 8, :].bitcast(I32),
                 )
-
-        def gather_words(name, table):
-            gathered = keep.tile([P, SLOTS], U32, name=name, align_bytes=64)
-            nc.vector.tensor_copy(gathered[:], table[:].indirect(offsets[:]))
-            return gathered
 
         def gather_words_in_halves(name, table):
             gathered = keep.tile([P, SLOTS], U32, name=name, align_bytes=64)
@@ -210,11 +205,12 @@ def tile_attend_plh_swiglu4_topk_kernel(tc, qT, k_words, k_scales, c_words, c_sc
                 out_1[0, :, at, :].rearrange("p n b -> p (n b)").bitcast(I32), y_codes[:, at].bitcast(I32)
             )
 
-        k_gathered = gather_words("k_gathered", k_table)
+        k_gathered = gather_words_in_halves("k_gathered", k_table)
         k_split = [keep.tile([P, split_bytes], U8, name="k_split%d" % pair, align_bytes=64) for pair in range(PAIRS)]
-        for pair in range(PAIRS):
-            split_words(k_split[pair], k_gathered, pair)
-        round_q(nc.vector.tensor_copy, LATE, 0, both)
+        split_words(k_split[0], k_gathered, 0, (slice(0, P // 2), slice(P // 2, P)))
+        split_words(k_split[1], k_gathered, 1)
+        round_q(nc.vector.tensor_copy, LATE, 0, slice(96, HALF))
+        round_q(nc.scalar.copy, LATE, 0, slice(0, 96))
         round_q(nc.scalar.copy, EARLY, 0, both)
         for h in (LATE, EARLY):
             quantise_q(h, 0, both)

@@ -52,18 +52,20 @@ def tile_attend_plh_swiglu4_topk_kernel(tc, qT, k_words, k_scales, c_words, c_sc
         nc.scalar.activation(warm[:, 1:2], warm[:, 0:1], SILU)
 
         scale_tables = []
-        for name, scales in (("k_scales", k_scales), ("c_scales", c_scales)):
+        for name, scales, rows in (("k_scales", k_scales, "o f t -> f o t"), ("c_scales", c_scales, "o f t -> (o f) t")):
             at = 2 * PACK * HALF * 4 - NEURONS // 2 if name == "k_scales" else 0
             table = placed.tile([P, NEURONS], U8, name=name, align_bytes=64, offset=at)
-            nc.sync.dma_start(table[SCALE_ROW0:P, :].bitcast(I32), scales.rearrange("o f t -> f o t").bitcast(I32))
+            nc.sync.dma_start(table[SCALE_ROW0:P, :].bitcast(I32), scales.rearrange(rows).bitcast(I32))
             nc.gpsimd.memset(table[0:SCALE_ROW0, :].bitcast(I32), 0)
             scale_tables.append(table)
 
-        planes = []
-        for w in (GATE, LAYER):
-            plane = keep.tile([P, PASSES, SLOTS], U8, name="planes%d" % w, align_bytes=64)
-            nc.vector.memset(plane[:].rearrange("p o s -> p (o s)").bitcast(I32), 0)
-            planes.append(plane)
+        gate_planes = keep.tile([P, PASSES, SLOTS], U8, name="gate_planes", align_bytes=64)
+        nc.vector.memset(gate_planes[:].rearrange("p o s -> p (o s)").bitcast(I32), 0)
+        planes = {(GATE, o): gate_planes[:, o, :] for o in range(PASSES)}
+        for o in range(PASSES):
+            plane = keep.tile([P, SLOTS], U8, name="layer_plane%d" % o, align_bytes=64)
+            nc.vector.memset(plane[:].bitcast(I32), 0)
+            planes[LAYER, o] = plane[:]
 
         def load_words(table, words):
             nc.sync.dma_start(table[:].bitcast(I32), words[0].rearrange("p t b -> p (t b)").bitcast(I32))
@@ -86,8 +88,16 @@ def tile_attend_plh_swiglu4_topk_kernel(tc, qT, k_words, k_scales, c_words, c_sc
             for quad in range(QUADS):
                 first_row = SCALE_ROW0 + 8 * quad
                 nc.sync.dma_start(
-                    planes[w][32 * quad : 32 * quad + 4].bitcast(I32),
+                    gate_planes[32 * quad : 32 * quad + 4].bitcast(I32),
                     dealt[first_row : first_row + 8, :].bitcast(I32),
+                )
+
+        def move_layer_scales(dealt, o):
+            for quad in range(QUADS):
+                first_row = SCALE_ROW0 + 16 * o + 4 * quad
+                nc.sync.dma_start(
+                    planes[LAYER, o][32 * quad : 32 * quad + 4, :].bitcast(I32),
+                    dealt[first_row : first_row + 4, :].bitcast(I32),
                 )
 
         def gather_words_in_halves(name, table):
@@ -107,7 +117,7 @@ def tile_attend_plh_swiglu4_topk_kernel(tc, qT, k_words, k_scales, c_words, c_sc
         split_bytes = 2 * PASSES * P * 2
 
         raw_bytes = PACK * HALF * 4
-        k_table = keep.tile([P, NEURONS], U32, name="k_table", align_bytes=64)
+        k_table = late_steps.tile([P, NEURONS], U32, name="k_table", align_bytes=64, offset=2304)
         load_words(k_table, k_words)
         raw0 = keep.tile([P, PACK, NQ], F32, name="q_raw0", align_bytes=64)
         nc.sync.dma_start(raw0[:], qT[0, 0:K_PASS, :].rearrange("(p j) n -> p j n", j=PACK))
@@ -117,7 +127,8 @@ def tile_attend_plh_swiglu4_topk_kernel(tc, qT, k_words, k_scales, c_words, c_sc
         c_table = placed.tile([P, NEURONS], U32, name="c_table", align_bytes=64, offset=2 * raw_bytes)
         load_words(c_table, c_words)
         load_q(early, EARLY, 1)
-        move_scales(LAYER, gather_scales(LAYER))
+        c_dealt = gather_scales(LAYER)
+        move_layer_scales(c_dealt, 0)
         late = placed.tile([P, PACK, HALF], F32, name="q_raw11", align_bytes=64, offset=0)
         load_q(late, LATE, 1)
         raw[EARLY, 1], raw[LATE, 1] = early[:], late[:]
@@ -131,8 +142,9 @@ def tile_attend_plh_swiglu4_topk_kernel(tc, qT, k_words, k_scales, c_words, c_sc
             for o in range(PASSES):
                 name = "q_codes%d%d" % (h, o)
                 q_codes[h, o] = keep.tile([P, HALF], U32, name=name, align_bytes=64)
-                if (h, o) == (EARLY, 1):
-                    q_scales[h, o] = late_steps.tile([P, HALF], U8, name="q_scales01", align_bytes=64, offset=1024)
+                if o == 1:
+                    at = 1024 if h == EARLY else 2304
+                    q_scales[h, o] = late_steps.tile([P, HALF], U8, name="q_scales%d1" % h, align_bytes=64, offset=at)
                 else:
                     q_scales[h, o] = keep.tile([P, HALF], U8, name="q_scales%d%d" % (h, o), align_bytes=64)
         y_codes = keep.tile([P, NQ], U32, name="y_codes", align_bytes=64)
@@ -163,7 +175,7 @@ def tile_attend_plh_swiglu4_topk_kernel(tc, qT, k_words, k_scales, c_words, c_sc
                 nc.tensor.matmul_mx(
                     out=banks[w, h, pair][:, i, :],
                     lhsT=words[pair][:, first : first + 2 * P].bitcast(FP4X4),
-                    lhsT_scale=planes[w][:, o, r * P : (r + 1) * P],
+                    lhsT_scale=planes[w, o][:, r * P : (r + 1) * P],
                     rhs=q_codes[h, o][:].bitcast(FP8X4),
                     rhs_scale=q_scales[h, o][:],
                     start=(o == opening and i == 0),
@@ -206,6 +218,9 @@ def tile_attend_plh_swiglu4_topk_kernel(tc, qT, k_words, k_scales, c_words, c_sc
             )
 
         k_gathered = gather_words_in_halves("k_gathered", k_table)
+        c_dealt_again = late_steps.tile([P, SLOTS], U8, name="c_scales_dealt_again", align_bytes=64, offset=2304)
+        nc.vector.tensor_copy(c_dealt_again[:].bitcast(I32), c_dealt[:].bitcast(I32))
+        move_layer_scales(c_dealt_again, 1)
         k_split = [keep.tile([P, split_bytes], U8, name="k_split%d" % pair, align_bytes=64) for pair in range(PAIRS)]
         split_words(k_split[0], k_gathered, 0, (slice(0, P // 2), slice(P // 2, P)))
         split_words(k_split[1], k_gathered, 1)
@@ -222,8 +237,8 @@ def tile_attend_plh_swiglu4_topk_kernel(tc, qT, k_words, k_scales, c_words, c_sc
             late_steps.tile([P, split_bytes], U8, name="c_split1", align_bytes=64, offset=1280),
         ]
         split_words(c_split[0], c_gathered, 0, (slice(0, P // 2), slice(P // 2, P)))
-        round_q(nc.scalar.copy, EARLY, 1, low)
-        round_q(nc.vector.tensor_copy, EARLY, 1, high)
+        round_q(nc.scalar.copy, EARLY, 1, slice(0, 176))
+        round_q(nc.vector.tensor_copy, EARLY, 1, slice(176, HALF))
         for h in (EARLY, LATE):
             bank_pass(c_split, LAYER, h, 0, 0)
         split_words(c_split[1], c_gathered, 1)

@@ -93,11 +93,11 @@ def tile_attend_plh_swiglu4_topk_kernel(tc, qT, k_words, k_scales, c_words, c_sc
                 )
 
         def move_layer_scales(dealt, o):
-            for quad in range(QUADS):
-                first_row = SCALE_ROW0 + 16 * o + 4 * quad
+            for j in range(4):
+                first_row = SCALE_ROW0 + 16 * o + j
                 nc.sync.dma_start(
-                    planes[LAYER, o][32 * quad : 32 * quad + 4, :].bitcast(I32),
-                    dealt[first_row : first_row + 4, :].bitcast(I32),
+                    planes[LAYER, o][j:P:32, :].bitcast(I32),
+                    dealt[first_row : SCALE_ROW0 + 16 * (o + 1) : 4, :].bitcast(I32),
                 )
 
         def gather_words_in_halves(name, table):

from contextlib import ExitStack

import concourse.mybir as mybir

NEURONS, D, NQ, SLOTS = 2048, 1024, 512, 512
FLOPS = 2 * 2 * SLOTS * D * NQ

F32 = mybir.dt.float32
BF16 = mybir.dt.bfloat16
I32 = mybir.dt.int32
U32 = mybir.dt.uint32
U16 = mybir.dt.uint16
U8 = mybir.dt.uint8
FP8X4 = mybir.dt.float8_e4m3fn_x4
FP4X4 = mybir.dt.float4_e2m1fn_x4
SILU = mybir.ActivationFunctionType.Silu
MULT = mybir.AluOpType.mult

P = 128
PACK = 4
K_PASS = P * PACK
PASSES = D // K_PASS
QUADS = 4
SCALE_ROW0 = P - 32
GATE, LAYER = 0, 1
HALF = NQ // 2
EARLY, LATE = 0, 1
PAIRS = 2


def interleave(copy, dst, src):
    copy(
        dst.rearrange("p (c i) t -> p c t i", i=4),
        src.rearrange("p t (c i) -> p c t i", i=4),
    )


def tile_attend_plh_swiglu4_topk_kernel(tc, qT, k_words, k_scales, c_words, c_scales, offs, out_0, out_1, out_2):
    nc = tc.nc
    with ExitStack() as ctx:
        lists = ctx.enter_context(tc.tile_pool(name="lists", bufs=1))
        keep = ctx.enter_context(tc.tile_pool(name="keep", bufs=1))
        placed = ctx.enter_context(tc.tile_pool(name="placed", bufs=1))
        late_steps = ctx.enter_context(tc.tile_pool(name="late_steps", bufs=1))
        psum = ctx.enter_context(tc.psum_pool(name="psum", bufs=1))

        offsets = lists.tile([P, SLOTS // 16], U16, name="offsets")
        nc.sync.dma_start(offsets[:], offs)

        warm = keep.tile([P, 2], F32, name="warm")
        nc.gpsimd.memset(warm[:, 0:1], 0.0)
        nc.scalar.activation(warm[:, 1:2], warm[:, 0:1], SILU)

        scale_tables = []
        for name, scales, rows in (("k_scales", k_scales, "o f t -> f o t"), ("c_scales", c_scales, "o f t -> (o f) t")):
            at = 2 * PACK * HALF * 4 - NEURONS // 2 if name == "k_scales" else 0
            table = placed.tile([P, NEURONS], U8, name=name, align_bytes=64, offset=at)
            nc.sync.dma_start(table[SCALE_ROW0:P, :].bitcast(I32), scales.rearrange(rows).bitcast(I32))
            nc.gpsimd.memset(table[0:SCALE_ROW0, :].bitcast(I32), 0)
            scale_tables.append(table)

        gate_planes = keep.tile([P, PASSES, SLOTS], U8, name="gate_planes", align_bytes=64)
        nc.vector.memset(gate_planes[:].rearrange("p o s -> p (o s)").bitcast(I32), 0)
        planes = {(GATE, o): gate_planes[:, o, :] for o in range(PASSES)}
        for o in range(PASSES):
            plane = keep.tile([P, SLOTS], U8, name="layer_plane%d" % o, align_bytes=64)
            nc.vector.memset(plane[:].bitcast(I32), 0)
            planes[LAYER, o] = plane[:]

        def load_words(table, words):
            nc.sync.dma_start(table[:].bitcast(I32), words[0].rearrange("p t b -> p (t b)").bitcast(I32))

        def load_q(raw, h, o):
            rows = qT[0, K_PASS * o : K_PASS * (o + 1), HALF * h : HALF * (h + 1)]
            nc.sync.dma_start(raw[:], rows.rearrange("(p j) n -> p j n", j=PACK))

        def gather_scales(w):
            if w == GATE:
                dealt = keep.tile([P, SLOTS], U8, name="k_scales_dealt", align_bytes=64)
            else:
                dealt = late_steps.tile([P, SLOTS], U8, name="c_scales_dealt", align_bytes=64, offset=960)
            nc.vector.tensor_copy(
                dealt[:].rearrange("p (r m) -> p m r", r=PACK), scale_tables[w][:].indirect(offsets[:])
            )
            return dealt

        def move_scales(w, dealt):
            for quad in range(QUADS):
                first_row = SCALE_ROW0 + 8 * quad
                nc.sync.dma_start(
                    gate_planes[32 * quad : 32 * quad + 4].bitcast(I32),
                    dealt[first_row : first_row + 8, :].bitcast(I32),
                )

        def move_layer_scales(dealt, o):
            for j in range(4):
                first_row = SCALE_ROW0 + 16 * o + j
                nc.sync.dma_start(
                    planes[LAYER, o][j:P:32, :].bitcast(I32),
                    dealt[first_row : SCALE_ROW0 + 16 * (o + 1) : 4, :].bitcast(I32),
                )

        def gather_words_in_halves(name, table):
            gathered = keep.tile([P, SLOTS], U32, name=name, align_bytes=64)
            for half in range(2):
                slots = slice(half * SLOTS // 2, (half + 1) * SLOTS // 2)
                entries = offsets[:, slots.start // 16 : slots.stop // 16]
                nc.vector.tensor_copy(gathered[:, slots], table[:].indirect(entries))
            return gathered

        def split_words(words, gathered, pair, pieces=(slice(0, P),)):
            halves = gathered[:].bitcast(U16).rearrange("p (m r o) -> p m r o", r=PACK, o=PASSES)
            by_slot = words[:].bitcast(U16).rearrange("p (r o m) -> p m r o", r=2, o=PASSES)
            for m in pieces:
                nc.vector.tensor_copy(by_slot[:, m], halves[:, m, 2 * pair : 2 * pair + 2, :])

        split_bytes = 2 * PASSES * P * 2

        raw_bytes = PACK * HALF * 4
        k_table = late_steps.tile([P, NEURONS], U32, name="k_table", align_bytes=64, offset=2304)
        load_words(k_table, k_words)
        raw0 = keep.tile([P, PACK, NQ], F32, name="q_raw0", align_bytes=64)
        nc.sync.dma_start(raw0[:], qT[0, 0:K_PASS, :].rearrange("(p j) n -> p j n", j=PACK))
        raw = {(h, 0): raw0[:, :, HALF * h : HALF * (h + 1)] for h in (EARLY, LATE)}
        move_scales(GATE, gather_scales(GATE))
        early = placed.tile([P, PACK, HALF], F32, name="q_raw10", align_bytes=64, offset=raw_bytes)
        c_table = placed.tile([P, NEURONS], U32, name="c_table", align_bytes=64, offset=2 * raw_bytes)
        load_words(c_table, c_words)
        load_q(early, EARLY, 1)
        c_dealt = gather_scales(LAYER)
        move_layer_scales(c_dealt, 0)
        late = placed.tile([P, PACK, HALF], F32, name="q_raw11", align_bytes=64, offset=0)
        load_q(late, LATE, 1)
        raw[EARLY, 1], raw[LATE, 1] = early[:], late[:]

        q_codes, q_scales, grouped = {}, {}, {}
        for h in (EARLY, LATE):
            for o in range(PASSES):
                name = "q_grouped%d%d" % (h, o)
                grouped[h, o] = keep.tile([P, HALF, PACK], BF16, name=name, tag=name, align_bytes=64)
        for h in (EARLY, LATE):
            for o in range(PASSES):
                name = "q_codes%d%d" % (h, o)
                q_codes[h, o] = keep.tile([P, HALF], U32, name=name, align_bytes=64)
                if o == 1:
                    at = 1024 if h == EARLY else 2304
                    q_scales[h, o] = late_steps.tile([P, HALF], U8, name="q_scales%d1" % h, align_bytes=64, offset=at)
                else:
                    q_scales[h, o] = keep.tile([P, HALF], U8, name="q_scales%d%d" % (h, o), align_bytes=64)
        y_codes = keep.tile([P, NQ], U32, name="y_codes", align_bytes=64)
        y_scales = keep.tile([P, NQ], U8, name="y_scales", align_bytes=64)
        low, high, both = slice(0, HALF // 2), slice(HALF // 2, HALF), slice(0, HALF)

        def round_q(copy, h, o, cols):
            interleave(copy, grouped[h, o][:, cols, :], raw[h, o][:, :, cols])

        def quantise_q(h, o, cols):
            nc.vector.quantize_mx(
                out=q_codes[h, o][:, cols].bitcast(FP8X4),
                scales=q_scales[h, o][:, cols],
                in_=grouped[h, o][:, cols, :].rearrange("p n t -> p (n t)"),
            )

        banks = {}
        for h in (EARLY, LATE):
            for w in (GATE, LAYER):
                for pair in range(PAIRS):
                    tag = "bank%d%d%d" % (w, h, pair)
                    banks[w, h, pair] = psum.tile([P, 2, HALF], F32, name="bank%d%d%d" % (w, h, pair), tag=tag)

        def bank_pass(words, w, h, pair, o, opening=0):
            for i in range(2):
                r = 2 * pair + i
                first = 2 * P * (PASSES * i + o)
                nc.tensor.matmul_mx(
                    out=banks[w, h, pair][:, i, :],
                    lhsT=words[pair][:, first : first + 2 * P].bitcast(FP4X4),
                    lhsT_scale=planes[w, o][:, r * P : (r + 1) * P],
                    rhs=q_codes[h, o][:].bitcast(FP8X4),
                    rhs_scale=q_scales[h, o][:],
                    start=(o == opening and i == 0),
                    stop=(o != opening and i == 1),
                )

        gate, y, y_grouped = {}, {}, {}
        for h in (EARLY, LATE):
            gate[h] = keep.tile([P, PACK, HALF], F32, name="gate%d" % h)
            y_grouped[h] = keep.tile([P, HALF, PACK], BF16, name="y_grouped%d" % h, align_bytes=64)
            if h == EARLY:
                y[h] = placed.tile([P, PACK, HALF], F32, name="y0", align_bytes=64, offset=0)
            else:
                y[h] = keep.tile([P, PACK, HALF], F32, name="y1")
        out_rows = out_0.rearrange("(p r) n -> p r n", r=PACK)

        def silu(h, pair):
            nc.scalar.activation(gate[h][:, 2 * pair : 2 * pair + 2, :], banks[GATE, h, pair][:], SILU)

        def product(h, pair):
            rows = slice(2 * pair, 2 * pair + 2)
            nc.vector.tensor_tensor(y[h][:, rows, :], banks[LAYER, h, pair][:], gate[h][:, rows, :], MULT)
            nc.sync.dma_start(out_rows[:, rows, HALF * h : HALF * (h + 1)], y[h][:, rows, :])

        def round_y(copy, h, cols):
            interleave(copy, y_grouped[h][:, cols, :], y[h][:, :, cols])

        def quantise_y(h, cols):
            at = slice(HALF * h + cols.start, HALF * h + cols.stop)
            nc.vector.quantize_mx(
                out=y_codes[:, at].bitcast(FP8X4),
                scales=y_scales[:, at],
                in_=y_grouped[h][:, cols, :].rearrange("p n t -> p (n t)"),
            )

        def store_codes(h):
            at = slice(HALF * h, HALF * (h + 1))
            nc.sync.dma_start(
                out_1[0, :, at, :].rearrange("p n b -> p (n b)").bitcast(I32), y_codes[:, at].bitcast(I32)
            )

        k_gathered = gather_words_in_halves("k_gathered", k_table)
        c_dealt_again = late_steps.tile([P, SLOTS], U8, name="c_scales_dealt_again", align_bytes=64, offset=2304)
        nc.vector.tensor_copy(c_dealt_again[:].bitcast(I32), c_dealt[:].bitcast(I32))
        move_layer_scales(c_dealt_again, 1)
        k_split = [keep.tile([P, split_bytes], U8, name="k_split%d" % pair, align_bytes=64) for pair in range(PAIRS)]
        split_words(k_split[0], k_gathered, 0, (slice(0, P // 2), slice(P // 2, P)))
        split_words(k_split[1], k_gathered, 1)
        round_q(nc.vector.tensor_copy, LATE, 0, slice(96, HALF))
        round_q(nc.scalar.copy, LATE, 0, slice(0, 96))
        round_q(nc.scalar.copy, EARLY, 0, both)
        for h in (LATE, EARLY):
            quantise_q(h, 0, both)
            for pair in range(PAIRS):
                bank_pass(k_split, GATE, h, pair, 0)
        c_gathered = gather_words_in_halves("c_gathered", c_table)
        c_split = [
            keep.tile([P, split_bytes], U8, name="c_split0", align_bytes=64),
            late_steps.tile([P, split_bytes], U8, name="c_split1", align_bytes=64, offset=1280),
        ]
        split_words(c_split[0], c_gathered, 0, (slice(0, P // 2), slice(P // 2, P)))
        round_q(nc.scalar.copy, EARLY, 1, slice(0, 176))
        round_q(nc.vector.tensor_copy, EARLY, 1, slice(176, HALF))
        for h in (EARLY, LATE):
            bank_pass(c_split, LAYER, h, 0, 0)
        split_words(c_split[1], c_gathered, 1)
        quantise_q(EARLY, 1, both)
        for pair in range(PAIRS):
            bank_pass(k_split, GATE, EARLY, pair, 1)
            silu(EARLY, pair)
        bank_pass(c_split, LAYER, EARLY, 0, 1)
        for o in range(PASSES):
            bank_pass(c_split, LAYER, EARLY, 1, o)
        for cols in (low, high):
            round_q(nc.vector.tensor_copy, LATE, 1, cols)
        for cols in (low, high):
            quantise_q(LATE, 1, cols)
        for pair in range(PAIRS):
            bank_pass(k_split, GATE, LATE, pair, 1)
            silu(LATE, pair)
        product(EARLY, 0)
        product(EARLY, 1)
        for pair in range(PAIRS):
            for o in (1,) if pair == 0 else (1, 0):
                bank_pass(c_split, LAYER, LATE, pair, o, opening=pair)
            product(LATE, pair)
        round_y(nc.scalar.copy, EARLY, both)
        round_y(nc.scalar.copy, LATE, slice(192, HALF))
        round_y(nc.vector.tensor_copy, LATE, slice(0, 192))
        quantise_y(EARLY, both)
        store_codes(EARLY)
        quantise_y(LATE, both)
        store_codes(LATE)
        for quad in range(QUADS):
            queue = nc.sync if quad >= QUADS // 2 else nc.scalar
            queue.dma_start(
                out_2[0, 4 * quad : 4 * quad + 4, :].bitcast(I32), y_scales[32 * quad : 32 * quad + 4, :].bitcast(I32)
            )
